import numpy as np, ml_dtypes
CORES = [3,7,11,15,131,135,139,143]
N = 8
BF = ml_dtypes.bfloat16
def gentries(a):
    return np.ascontiguousarray(a.reshape(8, 16, -1).transpose(0, 2, 1)).reshape(8, -1)
def gtable(e):
    e = np.asarray(e); return np.ascontiguousarray(e.reshape(8, -1, 16).transpose(0, 2, 1)).reshape(128, -1).astype(np.int32)
V, D, T, RO, NEED = 1152, 2, 32, 2, 9
E = D * V
def graph(rng, sizes, kinds, stray):
    c = rng.choice(np.array(sizes), V); z = np.add.accumulate(c); i = np.arange(V)
    b = np.searchsorted(z, i, side="right"); a = (z - c)[b]; n = np.minimum(z[b], V) - a
    kind = rng.choice(np.array(kinds), V)[b]; back = a + np.where(kind == 2, rng.integers(0, n), 0)
    t = np.where(kind == 0, a + rng.integers(0, n, (D, V)), np.where(i + 1 < a + n, i + 1, back))
    t = np.where(rng.random((D, V)) < stray, rng.integers(0, V, (D, V)), t)
    line = rng.permutation(V); h = np.empty((D, V), np.int64); h[:, line] = line[t]
    q = np.empty((3, V), np.int64); q[:, line] = np.stack([b, i - a, n])
    return h, q
def spins(rng, lean):
    return np.minimum(np.maximum(rng.integers(-7, 8, (16, E)) + np.tile(lean, D), -7), 7)
def sevens(rng, *shape):
    return np.where(rng.random(shape) < 0.125, 6, 7)
def layers(rng, sizes, kinds, strays, step):
    x = np.empty((N, 8, 16, E), np.int64); h = np.empty((N, 8, D, V), np.int64)
    for r in range(N):
        for g in range(8):
            h[r, g], q = graph(rng, sizes, kinds, rng.choice(np.array(strays)))
            x[r, g] = spins(rng, rng.integers(-step, step + 1, V)[q[0]])
    return x, np.argsort(rng.random((N, 8, E)), axis=-1), h
def pack(x, o, h):
    s = np.empty((N, 8, 16, E), np.int64); np.put_along_axis(s, np.ascontiguousarray(np.broadcast_to(o[:, :, None, :], s.shape)), x, 3)
    e = np.empty((N, 8, E), np.int64); np.put_along_axis(e, o, h.reshape(N, 8, E), 2)
    return {"sp": s.reshape(N, 128, E).astype(np.float32).astype(BF), "lv": np.stack([gtable(a) for a in o]), "hd": e.astype(np.int32)}
SIZES = (1, 2, 3, 5, 8, 13, 21, 34, T, T + 9)
def setup_inputs(rng):
    return pack(*layers(rng, SIZES, (0, 0, 0, 1, 1, 2), (0.0, 0.01, 0.04), 2))
def setup_inputs_length(rng):
    x, o, h = layers(rng, (1, T // 2, T - 1, T, T, T + 1, T + 1, 2 * T, 3 * T), (1, 1, 2), (0.0,), 3)
    for r in (0, N - 1):
        for g, c in enumerate((T, T + 1, T - 1, 2 * T, T // 2 + 1, 2, 256 + T // 2)):
            h[r, g], q = graph(rng, (c,), (1,), 0.0); x[r, g] = spins(rng, np.full(V, 3))
        line = np.concatenate([np.zeros(1, np.int64), 1 + rng.permutation(V - 1)]); to = np.empty(V, np.int64)
        to[line[1:]] = line[:-1]; to[0] = line[rng.integers(0, T // 2)]
        h[r, 7] = to; x[r, 7] = rng.integers(1, 8, (16, E))
    return pack(x, o, h)
def setup_inputs_verdict(rng):
    x, o, h = layers(rng, (1,), (1,), (0.0,), 0)
    for r in range(N):
        for g in range(8):
            h[r, g], q = graph(rng, (1, 2, 3, 4, 5, 8, 16), (1,), 0.0); b, j, n = q
            amp = rng.integers(-6, 7, (16, V))[:, b]; y = np.where(j % 2 == 1, -amp, amp)
            y = np.where((n % 2 == 1) & (j == n - 1), 0, y)
            won = np.argsort(rng.random((16, V)), axis=0) < rng.choice(np.array([NEED - 1, NEED, NEED, 0, 16]), V)
            want = np.where(won, 1, -rng.integers(0, 2, (16, V)))[:, b]
            x[r, g] = np.tile(y + np.where(j == 0, want, 0), (1, D))
    return pack(x, o, h)
def setup_inputs_ties(rng):
    x, o, h = layers(rng, (1, 2, 3, 5, 8), (0, 0, 1), (0.0, 0.01), 0)
    x[:, :2] = rng.choice(np.array([-7, -1, 0, 1, 2]), (N, 2, 1, E)); x[:, 2:4] = rng.integers(-1, 2, (N, 2, 16, E))
    x[:, 4:] = rng.integers(5, 8, (N, 4, 16, E)); near = np.array([7] * 6 + [5] * 7 + [6] * 3)
    for g in range(4, 8):
        y = x[:, g]; v = rng.permutation(V)[:V // 16]
        y[:, :, v] = 6; y[:, :, V + v] = rng.permutation(near)[:, None]
        for k in range(2, D): y[:, :, k * V + v] = 5
    x[:, 5::2] = -x[:, 5::2]
    return pack(x, o, h)
def setup_inputs_alike(rng):
    x, o, h = layers(rng, SIZES, (0, 1, 2), (0.0, 0.02), 2); i = np.arange(V)
    h[:, 0] = i; h[:, 1] = i ^ 1; h[:, 2] = 0; h[:, 3] = V - 1; h[:, 4] = np.roll(i, -1); h[:, 5] = rng.choice(np.array([0, V - 1]), (N, D, V))
    o[:, 6] = np.arange(E); o[:, 7] = np.arange(E)[::-1]
    r = int(rng.integers(0, N)); h[r] = i
    x[r] = sevens(rng, 8, 16, E); x[(r + 1) % N] = -sevens(rng, 8, 16, E); x[(r - 1) % N, :2] = sevens(rng, 2, 16, E)
    return pack(x, o, h)
def setup_inputs_spread(rng):
    x, o, h = layers(rng, (1, 2, 3, 4, 6, 9, 30), (0, 0, 1, 2), (0.0, 0.02), 0)
    size = rng.choice(np.array([0, 1, 1, 3, 7, 7]), (N, 8, 1, E)); sign = rng.choice(np.array([-1, 0, 1]), (N, 8, 1, E))
    v = np.rint((2 * rng.random((N, 8, 16, E)) - 1) * size).astype(np.int64)
    return pack(np.where(sign == 0, v, sign * np.abs(v)), o, h)
def check_inputs(d):
    bad = []; s = np.asarray(d["sp"]).astype(np.float32)
    if not (np.all(np.abs(s) <= 7) and np.all(s == np.rint(s))): bad.append("whole numbers of sp")
    if any(np.any(np.sort(gentries(a), axis=1) != np.arange(E)) for a in d["lv"]): bad.append("each edge once in lv")
    if np.min(d["hd"]) < 0 or np.max(d["hd"]) > V - 1: bad.append("range of hd")
    return bad
def reference(sp, lv, hd):
    s = sp.astype(np.float32).astype(np.int64).reshape(N, 8, 16, E); h = hd.astype(np.int64)
    o = np.stack([gentries(a) for a in lv]).astype(np.int64); me = np.arange(V); w = np.zeros((N, 8, 16, V), np.int64)
    for rnd in range(RO):
        so = np.take_along_axis(s, o[:, :, None, :], 3)
        a = np.add.reduce(so * np.roll(so, -1, axis=0), axis=2).reshape(N, 8, D, V)
        slot = np.argmax(a, axis=2) * V + me
        c = np.take_along_axis(o, slot, 2); nx = np.take_along_axis(h, c, 2)
        m = np.take_along_axis(so, slot[:, :, None, :], 3); low = nx; p = nx; n = 1
        while n < T:
            m = m + np.take_along_axis(m, p[:, :, None, :], 3); low = np.minimum(low, np.take_along_axis(low, p, 2)); p = np.take_along_axis(p, p, 2); n = 2 * n
        w = w + m
        r, g, v = np.nonzero((low == me) & (np.add.reduce((m > 0).astype(np.int64), axis=2) >= NEED))
        turn = np.zeros((N, 8, V), bool)
        for j in range(T):
            turn[r, g, v] = True; v = nx[r, g, v]
        r, g, v = np.nonzero(turn); u = nx[r, g, v]; e = c[r, g, v]
        o[r, g, slot[r, g, u]] = e; h[r, g, e] = v; s[r, g, :, e] = -s[r, g, :, e]
    return {"ys": s.reshape(N, 128, E).astype(np.float32).astype(BF), "yl": o.astype(np.float32), "yh": h.astype(np.float32), "yw": w.reshape(N, 128, V).astype(np.float32)}

@@ -1,0 +1,723 @@
+from concourse.mybir import AluOpType as ALU, ActivationFunctionType as AF
+
+V = 1152
+E = 2304
+CH = 384
+BIG = 32768.0
+FAR = 1e6
+BF, F32, F16, I32, U16 = "bfloat16", "float32", "float16", "int32", "uint16"
+EST = dict(cyc=1.04, gath=1.55, scat=3.8, pe=0.6, wake=100, link=80.0, rounds=250, sig=1500.0, win=4000.0, seed=1)
+CFG = dict(
+    ha=36,
+    sc=(0, 12, 24, 36, 48, 60, 72),
+    nv=1,
+    xc=(0, 24, 52, 72),
+    vsv=(0, 30),
+    ysc=(1, 3, 5),
+)
+
+SB = {
+    "spb": (E, BF), "lvi": (144, I32), "lvu": (144, U16),
+    "hdi": (288, I32), "hdd": (576, I32), "hdb": (576, BF),
+    "et": (E, BF), "ct": (V, BF), "cc": (V, BF), "tab": (2 * E, BF), "ew": (E + V, BF),
+    "a16": (V, BF), "xo": (V, BF), "xn": (V, BF), "h192": (V, BF), "hi": (V, BF),
+    "pa16": (V, F16), "pb16": (V, F16), "sow": (E + V, BF), "nsw": (E + V, BF), "so": (E, BF), "ng": (E, BF), "pr2": (E, BF),
+    "p0a": (V, BF), "p0b": (V, BF), "p1": (V, BF), "p2": (V, BF), "pq": (V, BF), "p3": (V, BF), "p4": (V, BF), "p5": (V, BF),
+    "ma": (V, BF), "mb": (V, BF), "ma2": (V, BF), "mb2": (V, BF), "m5a": (V, BF), "m5b": (V, BF),
+    "yy": (V, F32), "ta": (V, F32), "tb": (V, F32), "aa": (V, F32), "ff": (V, F16),
+    "eq": (V, BF), "pp": (V, F16), "vs": (V, BF), "yg": (E, BF), "yso": (E, BF),
+    "lst": (72 * 12, U16), "msgo": (144, U16), "msgi": (144, U16), "ylu": (144, U16),
+    "wf": (72 * 64, F32), "wi": (72 * 10, I32), "ind": (144, BF),
+    "pi": (4, I32), "col": (64, F32), "oh": (16, F32), "jf": (144, F32), "jb": (128, BF), "b128": (18, F32),
+    "cb1": (18, F32), "cb2": (18, F32), "cb3": (18, F32), "dd": (128 * 5, BF),
+    "zb": (144 * 6, BF), "zh": (144 * 3, F16), "mb16": (128 * 17, BF), "mh16": (128 * 2, F16), "i16": (72, F32),
+}
+SCRATCH = {k: ("sbuf", [128, n], d) for k, (n, d) in SB.items()}
+SCRATCH.update({"psa": ("psum", [128, 1536], F32), "psb": ("psum", [128, 1536], F32),
+                "w0": ("psum", [128, 512], F32), "w1": ("psum", [128, 512], F32)})
+PSUM = ("psa", "psb", "w0", "w1")
+NDMA = 24
+SEMAPHORES = (["cv", "ca", "cp", "cg", "lsent", "ax0", "ax1", "ax2", "aso", "am0", "amsg"]
+              + ["d%d" % i for i in range(NDMA)])
+
+
+def rank_program(g, core, T, topo):
+    rank = T.rank_of(core)
+    if rank is None:
+        return
+    n = len(T.cores)
+    prev, nxt = T.cores[(rank - 1) % n], T.cores[(rank + 1) % n]
+    rid, pid = topo.addr(prev, core)
+    out_mask, n_out, n_in = topo.mask(core, prev), len(topo.engines(core, prev)), len(topo.engines(nxt, core))
+
+    ops = []
+    CYC = EST["cyc"]
+
+    def R(name, lo=0, hi=None, step=1, p=None):
+        return (name, lo, SB[name][0] if hi is None else hi, step, p)
+
+    def sub(r, lo, hi):
+        return (r[0], r[1] + lo, r[1] + hi, 1, None)
+
+    def tag(name, k=0):
+        return (name, k, k + 1, 1, None)
+
+    def ap(r):
+        name, lo, hi, step, p = r
+        ps = slice(None) if p is None else slice(*p)
+        return T[name][ps, lo:hi] if step == 1 else T[name][ps, lo:hi:step]
+
+    def span(r):
+        if r[0] in PSUM:
+            return (r[0], r[1] // 512 * 512, (r[2] + 511) // 512 * 512)
+        return r[:3]
+
+    def width(r):
+        return (r[2] - r[1] + r[3] - 1) // r[3]
+
+    def two(*rs):
+        return all(r[0] in SB and SB[r[0]][1] in (BF, F16, U16) for r in rs)
+
+    def cost(in0, per, idx=None, oidx=None):
+        if oidx is not None:
+            return 50 + 16 * width(oidx) * EST["scat"] * CYC
+        if idx is not None:
+            return 60 + 16 * width(idx) * EST["gath"] * CYC
+        return max(64, per * width(in0)) * CYC
+
+    def op(q, fn, reads, writes, kind="c", **kw):
+        rd = [span(r) for r in reads if r[0] not in PSUM]
+        wr = [span(r) for r in writes] + [span(r) for r in reads if r[0] in PSUM]
+        ops.append(dict(q=q, fn=fn, rd=rd, wr=wr, kind=kind, **kw))
+
+    def sc(x):
+        return ap(x) if isinstance(x, tuple) else x
+
+    def aps(*xs):
+        return [x for x in xs if isinstance(x, tuple)]
+
+    def src(x, idx):
+        return ap(x) if idx is None else ap(x).indirect(ap(idx))
+
+    def ts(out, in0, s1, s2, o0, o1=None, idx=None):
+        if o1 is None:
+            f = lambda: g.vector.tensor_scalar(ap(out), src(in0, idx), sc(s1), None, o0)
+        else:
+            f = lambda: g.vector.tensor_scalar(ap(out), src(in0, idx), sc(s1), sc(s2), o0, o1)
+        op("v", f, aps(in0, s1, s2, idx), [out], t=cost(in0, 0.5 if two(out, in0) else 1, idx))
+
+    def tt(out, in0, in1, o, idx=None, oidx=None, extra=()):
+        op("v", lambda: g.vector.tensor_tensor(src(out, oidx), src(in0, idx), ap(in1), o),
+           aps(in0, in1, idx, oidx) + list(extra), [out],
+           t=cost(in0, 1 if in0[0] in PSUM or in1[0] in PSUM else 2, idx, oidx))
+
+    def cp(out, in_, idx=None):
+        op("v", lambda: g.vector.tensor_copy(ap(out), src(in_, idx)), aps(in_, idx), [out],
+           t=cost(in_, 0.5 if two(out, in_) else 1, idx))
+
+    def cvt(out, in_):
+        ts(out, in_, 0.25, None, ALU.add)
+
+    def act(out, in_, func=AF.Identity, bias=0.0, scale=1.0, idx=None):
+        op("a", lambda: g.scalar.activation(ap(out), src(in_, idx), func, bias=sc(bias), scale=sc(scale)),
+           aps(in_, bias, scale, idx), [out], t=cost(in_, 1, idx))
+
+    def mm(out, lhsT, rhs, start, stop):
+        op("p", lambda: g.tensor.matmul(ap(out), ap(lhsT), ap(rhs), start, stop), [lhsT, rhs], [out],
+           t=max(64, width(rhs)) * EST["pe"])
+
+    def iota(out, pattern, base, cm, after=()):
+        if SB[out[0]][1] == I32:
+            f = lambda: g.iota(ap(out), pattern, base, cm)
+        else:
+            f = lambda: g.iota(ap(out), pattern, base, cm, allow_small_or_imprecise_dtypes=True)
+        op("g", f, list(after), [out], t=130 + 2 * width(out) * CYC)
+
+    def gcopy(out, in_):
+        op("g", lambda: g.affine_select(ap(out), ap(in_), [[0, in_[2] - in_[1]]], ALU.is_ge, 0.0, 0, 0), [in_], [out],
+           t=170 + 2 * width(out) * CYC)
+
+    def dma(q, o, i, reads, writes, add=False, lat=2600):
+        eng = {"g": g, "s": g.sync, "a": g.scalar}[q]
+        f = (lambda: eng.dma_start(o, i, accum_op=ALU.add)) if add else (lambda: eng.dma_start(o, i))
+        op(q, f, reads, writes, kind="d", t=400 if q == "g" else 100, lat=lat)
+
+    def send(dst, srcr, sem):
+        op("g", lambda: g.remote_dma(ap(dst), ap(srcr), T.sem[sem], T.sem.lsent, pid, rid, out_mask), [srcr], [], kind="r",
+           t=400, sem=sem, lat=2700 + width(srcr) * 256 / EST["link"])
+
+    def arrive(dst, sem):
+        op("x", None, [], [dst], kind="x", sem=sem, t=0)
+
+    def PS(name, j, w=CH):
+        return (name, 512 * j, 512 * j + w, 1, None)
+
+    def W(name, k=0, w=72):
+        return (name, 72 * k, 72 * k + w, 1, None)
+
+    def ch(name, j, base=0):
+        return R(name, base + CH * j, base + CH * (j + 1))
+
+    def cols(name, lo, hi, base=0):
+        return R(name, base + 16 * lo, base + 16 * hi)
+
+    def third(lst, j):
+        return sub(lst, 24 * j, 24 * j + 24)
+
+    def C(i):
+        return R("col", i, i + 1)
+
+    def OH(i):
+        return R("oh", i, i + 1)
+
+    slots = {}
+
+    def F(name, w=1):
+        if name not in slots:
+            slots[name] = sum(x[1] for x in slots.values()), w
+        lo, w = slots[name]
+        return R("wf", 72 * lo, 72 * (lo + w))
+
+    def half(r, k):
+        return sub(r, 72 * k, 72 * k + 72)
+
+    def MB(i):
+        return R("mb16", 128 * i, 128 * (i + 1))
+
+    def ZR(z):
+        return R(z[0], z[1], z[1] + 144)
+
+    def zsel(z, i):
+        return (z[0], z[1] + 15 - i, z[1] + 143 - i, 1, None)
+
+    def wrap(out, z, data, base, start=True, stop=True):
+        for i in range(16):
+            mm(out, zsel(z, i), R(data, base + i, base + V, 16), start and i == 0, stop and i == 15)
+
+    PARTS = ((0, CFG["ha"]), (CFG["ha"], 72))
+    ZONE, ZHEAD, ZEDGE, ZPTR, ZNEG, ZH89 = [("zb", 144 * i) for i in range(6)]
+    ZONE16, ZLOWA, ZLOWB = [("zh", 144 * i) for i in range(3)]
+    (PF, RF, C15, HV, TV, EV, LOWA, LOWB, A2, D13, GS, YB, B3, LT12, LT8, LT6, P1C, NTV, W67, R1, RH, TA, WA, OFF,
+     T0, T1, T2, T3, T4, T5, T6, T7, T8) = [C(i) for i in range(33)]
+    (DNI, DI, D16, D15, MA1A, MA1B, MA2, MX2, MX3, MOFF, MY, ME0, MS4, MS5, MSG, MT1, MT2) = range(17)
+    DD, DN, DM, D8N, D8 = [R("dd", 128 * i, 128 * i + 128) for i in range(5)]
+    for nm in ("slot", "slotm", "hs", "hs2", "fl", "mk", "q", "qm", "u", "u2", "sl", "tl", "base", "mkn"):
+        F(nm, 2)
+    LT, LC, L1, L2, L4, L8, L16, LL, LP, LE1, LE2 = [R("lst", 72 * i, 72 * i + 72) for i in range(11)]
+    mask, fl = half(F("mk"), 1), F("fl")
+
+    sp0 = R("spb")
+    dma("s", T.spb[:], T.sp[:], [], [sp0], lat=4800)
+    dma("a", T.hdi[0:64, :], T.hd[:], [], [R("hdi")])
+    dma("a", T.lvi[:], T.lv[:], [], [R("lvi")])
+
+    iota(R("pi", 0, 1), [[0, 1]], 0, 1)
+    iota(R("jf"), [[1, 144]], 0, 0)
+    iota(R("b128"), [[128, 18]], 0, 0)
+    iota(R("jb"), [[1, 128]], 0, 0)
+    iota(R("i16"), [[16, 72]], 0, 0)
+    ts(R("pi", 1, 2), R("pi", 0, 1), 15, None, ALU.bitwise_and)
+    cp(PF, R("pi", 0, 1))
+    ts(R("pi", 2, 3), R("pi", 0, 1), 1, None, ALU.bitwise_and)
+    cp(RF, R("pi", 1, 2))
+    ts(R("pi", 3, 4), R("pi", 1, 2), 1, None, ALU.logical_shift_right)
+    ts(R("oh"), R("jf", 0, 16), RF, None, ALU.is_equal)
+    ts(C15, PF, RF, 15.0, ALU.subtract, ALU.add)
+    ts(HV, RF, 4.0, 0.5, ALU.is_lt, ALU.mult)
+    ts(T0, OH(4), OH(8), OH(9), ALU.add, ALU.add)
+    act(A2, OH(2), bias=OH(0), scale=-1.0)
+    act(D13, OH(3), bias=OH(1), scale=-1.0)
+    ts(R("cb3"), R("b128"), OH(9), OH(4), ALU.mult, ALU.subtract)
+    ts(R("cb1"), R("b128"), OH(6), T0, ALU.mult, ALU.add)
+    ts(TV, RF, 2.0, HV, ALU.is_lt, ALU.subtract)
+    act(R("cb2"), R("b128"), scale=D13)
+    for b in range(9):
+        act(R("et", 128 * b, 128 * b + 128), R("jb"), bias=R("cb1", b, b + 1), scale=OH(5))
+    for b in range(9, 18):
+        ts(R("et", 128 * b, 128 * b + 128), R("jb"), OH(5), R("cb1", b, b + 1), ALU.mult, ALU.add)
+    cp(R1, R("pi", 2, 3))
+    cp(RH, R("pi", 3, 4))
+    ts(DD, R("jb"), C15, 15.0, ALU.subtract, ALU.add)
+    ts(LT12, RF, 12.0, None, ALU.is_lt)
+    ts(LT8, RF, 8.0, None, ALU.is_lt)
+    ts(LT6, RF, 6.0, None, ALU.is_lt)
+    ts(DN, DD, 0.0, 200.0, ALU.is_lt, ALU.mult)
+    hp = (0, 64)
+    ts(R("hdd", 0, 288, 1, hp), R("hdi", 0, 288, 1, hp), 127, None, ALU.bitwise_and)
+    ts(R("hdd", 288, 576, 1, hp), R("hdi", 0, 288, 1, hp), 0xF80, None, ALU.bitwise_and)
+    cp(R("lvu"), R("lvi"))
+    cp(R("hdb", 0, 576, 1, hp), R("hdd", 0, 576, 1, hp))
+    for r in range(4):
+        dma("s", T.et[r::16, :], T.hdb[0:64, 288 * (r % 2):288 * (r % 2) + 288], [R("hdb"), R("et")], [tag("etrow", r)])
+    etrows = [tag("etrow", r) for r in range(4)]
+    for i, w in ((DNI, -1.0), (DI, 1.0), (D16, 16.0), (D15, -15.9375)):
+        ts(MB(i), R("jb"), PF, w, ALU.is_equal, ALU.mult)
+    for b in range(9):
+        act(R("ct", 128 * b, 128 * b + 128), R("jb"), bias=R("cb2", b, b + 1), scale=A2)
+    for b in range(9):
+        act(R("cc", 128 * b, 128 * b + 128), R("jb"), bias=R("cb3", b, b + 1), scale=OH(8))
+    ts(ZR(ZHEAD), R("jf"), C15, HV, ALU.is_equal, ALU.mult)
+    ts(ZR(ZONE16), R("jf"), C15, None, ALU.is_equal)
+    act(half(F("slot"), 0), R("i16"), bias=RF)
+    act(half(F("slot"), 1), half(F("slot"), 0), bias=float(V))
+    act(F("dump"), half(F("slot"), 0), bias=float(E))
+    act(F("dump2"), half(F("slot"), 0), bias=float(E + V))
+    act(F("dumpm"), half(F("slot"), 0), bias=float(E - 8192))
+    act(F("slotm"), F("slot"), scale=-1.0)
+    tt(DM, DD, DN, ALU.add)
+    act(EV, OH(5), bias=OH(6))
+    act(TA, OH(8), bias=R1, scale=8.0)
+    act(WA, TV, bias=OH(8))
+    act(T2, R1, bias=2.0)
+    act(T3, R1, bias=4.0)
+    act(T4, R1, bias=6.0)
+    act(W67, OH(6), bias=OH(7))
+    act(T5, RH, bias=4.0)
+    act(T6, RH, bias=12.0)
+    act(T7, RH, bias=13.0)
+    act(OFF, OH(8), scale=2048.0)
+    act(YB, LT12, scale=BIG)
+    act(B3, LT8, bias=YB, scale=-(BIG + 2048.0))
+    act(NTV, TV, scale=-1.0)
+    act(P1C, PF, bias=1.0)
+    act(LOWA, OH(13), bias=OH(12), scale=2048.0)
+    act(LOWB, OH(15), bias=OH(14), scale=2048.0)
+    act(T8, OH(8), bias=OH(9))
+    ts(T1, OH(2), OH(3), OH(4), ALU.add, ALU.add)
+    act(GS, T1, bias=1.0, scale=-2.0)
+    ts(D8N, DM, 8.0, -8.0, ALU.is_ge, ALU.mult)
+    tt(D8, DM, D8N, ALU.add)
+    for z, w in ((ZEDGE, EV), (ZPTR, W67), (ZLOWA, LOWA), (ZLOWB, LOWB), (ZNEG, -4096.0), (ZH89, T8), (ZONE, 1.0)):
+        ts(ZR(z), R("jf"), C15, w, ALU.is_equal, ALU.mult)
+    for m, d, at, w in ((MT1, DM, T3, TV), (MT2, DM, T4, HV), (MA1A, DM, TA, WA), (MA1B, DM, T2, HV), (MY, DM, T6, LT8),
+                        (MX2, D8, RH, LT8), (MX3, D8, T5, LT8), (MS4, DM, 0.0, W67), (MS5, DM, T7, LT6)):
+        ts(MB(m), d, at, w, ALU.is_equal, ALU.mult)
+    tt(MB(MA2), MB(MT1), MB(MT2), ALU.add)
+    for m, below, w in ((MOFF, 8.0, OFF), (ME0, 16.0, NTV), (MSG, 16.0, OH(4))):
+        ts(MB(m), DM, below, w, ALU.is_lt, ALU.mult)
+    ts(R("mh16", 0, 128), R("jb"), PF, LT12, ALU.is_equal, ALU.mult)
+    ts(R("mh16", 128, 256), R("jb"), P1C, LT12, ALU.is_equal, ALU.mult)
+    for rd in range(2):
+        if CFG["vsv"][rd]:
+            ts(half(R("ind"), rd), R("jf", 0, 72), 72.0 - CFG["vsv"][rd], 65536.0, ALU.is_ge, ALU.mult)
+
+    XC = list(zip(CFG["xc"][:-1], CFG["xc"][1:]))
+    for j, (lo, hi) in enumerate(XC):
+        act(cols("a16", lo, hi), sp0, scale=16.0, idx=R("lvu", 72 + lo, 72 + hi))
+        tt(cols("xo", lo, hi), sp0, cols("a16", lo, hi), ALU.add, idx=R("lvu", lo, hi))
+        send(cols("xn", lo, hi), cols("xo", lo, hi), "ax%d" % j)
+
+    def xps(name, j):
+        return PS(name, j, 16 * (XC[j][1] - XC[j][0]))
+    for j, (lo, hi) in enumerate(XC):
+        mm(xps("psa", j), MB(DNI), cols("xo", lo, hi), True, False)
+        mm(xps("psa", j), MB(DI), cols("a16", lo, hi), False, True)
+        mm(xps("psb", j), MB(D16), cols("xo", lo, hi), True, False)
+        mm(xps("psb", j), MB(D15), cols("a16", lo, hi), False, True)
+    act(R("sow", V, E), R("a16"), scale=0.0625)
+    for j, (lo, hi) in enumerate(XC):
+        act(cols("sow", lo, hi), xps("psa", j), scale=-1.0)
+    for k in range(2):
+        for lo, hi in PARTS:
+            tt(cols("tab", lo, hi, V * k), R("et"), cols("ct", lo, hi), ALU.add, idx=R("lvu", 72 * k + lo, 72 * k + hi), extra=etrows)
+        wrap(W("w0", k), ZHEAD, "tab", V * k)
+    iota(R("ew", 0, 768), [[0, 768]], 1, 0, after=[R("xo")])
+    send(R("nsw", 0, E), R("sow", 0, E), "aso")
+    iota(R("ew", 768, E + V), [[0, E + V - 768]], 1, 0, after=[R("sow", 0, E), R("ew", 0, 768)])
+    for r in range(2):
+        dma("s", T.ew[8 + r::16, 0:E], T.hdb[0:64, 288 * r:288 * r + 288], [R("hdb")], [R("ew")])
+
+    for j, (lo, hi) in enumerate(XC):
+        arrive(cols("xn", lo, hi), "ax%d" % j)
+    for j, (lo, hi) in enumerate(XC):
+        act(cols("h192", lo, hi), cols("xn", lo, hi), bias=192.0, scale=0.0625)
+        act(cols("hi", lo, hi), cols("h192", lo, hi), bias=-192.0)
+        tt(cols("pa16", lo, hi), xps("psa", j), cols("xn", lo, hi), ALU.mult)
+        tt(cols("pb16", lo, hi), xps("psb", j), cols("hi", lo, hi), ALU.mult)
+    wrap(W("w1"), ZONE16, "pa16", 0, True, False)
+    wrap(W("w1"), ZONE16, "pb16", 0, False, True)
+    cp(F("hs"), W("w0", 0, 144))
+    tt(F("dH"), half(F("hs"), 1), half(F("hs"), 0), ALU.subtract)
+    ts(F("t0"), W("w1"), 0.0, float(V), ALU.is_gt, ALU.mult)
+    ts(mask, W("w1"), 0.0, None, ALU.is_gt)
+    tt(F("t3"), F("t0"), half(F("slot"), 0), ALU.add)
+    tt(F("t2"), mask, F("dH"), ALU.mult)
+    cp(LT, F("t3"))
+    tt(F("t5"), F("t2"), half(F("hs"), 0), ALU.add)
+
+    def scatter(p0, le, lo, hi):
+        tt(R("ew"), cols(p0, lo, hi), cols("cc", lo, hi), ALU.mult, oidx=sub(le, lo, hi))
+
+    def mstep(out, win, dup, idx, o=ALU.add, copy=None):
+        for lo, hi in PARTS:
+            tt(cols(out, lo, hi), R(win), sub(dup, 16 * lo, 16 * hi), o, idx=sub(idx, lo, hi))
+            if copy:
+                gcopy(cols(copy, lo, hi), cols(out, lo, hi))
+
+    def walk(rd):
+        p0, m5 = ("p0a", "m5a") if rd == 0 else ("p0b", "m5b")
+        act(R(p0), R("tab", 0, E + V * rd), idx=LT)
+        cvt(L1, F("t5"))
+        act(R("p1"), R(p0), idx=L1)
+        wrap(W("w1"), ZEDGE, p0, 0)
+        if rd == 0:
+            cp(R("ma"), R("sow", 0, E), idx=LT)
+            ts(R("sow", E, E + V), R("ma"), -1.0, None, ALU.mult)
+            send(R("nsw", E, E + V), R("sow", E, E + V), "am0")
+        else:
+            for lo, hi in PARTS:
+                cp(cols("ma", lo, hi), R("sow"), idx=sub(LC, lo, hi))
+                gcopy(cols("ma2", lo, hi), cols("ma", lo, hi))
+        wrap(W("w0"), ZHEAD, "p1", 0)
+        tt(F("dce"), W("w1"), F("dump"), ALU.subtract)
+        ts(half(F("mk"), 0), mask, -1.0, 1.0, ALU.mult, ALU.add)
+        if rd == 0:
+            ts(F("mkn"), F("mk"), -FAR, FAR, ALU.mult, ALU.add)
+        else:
+            for h in range(2):
+                tt(half(F("u2"), h), F("dump2"), half(F("tl"), h), ALU.subtract)
+            tt(F("q"), F("u2"), F("mk"), ALU.mult)
+            tt(F("t7"), F("dce"), F("dumpm"), ALU.add)
+        cp(L2, W("w0"))
+        for j in range(3):
+            mm(PS("psa", j), MB(MA1A), ch("p1", j), True, False)
+            mm(PS("psa", j), MB(MA1B), ch("p1", j), False, False)
+        act(R("p2"), R("p1"), idx=L2)
+        if rd == 0:
+            mstep("mb", "ma", R("sow", E, E + V), L1, o=ALU.subtract, copy="mb2")
+        else:
+            mstep("mb", "ma", R("ma2"), L1, copy="mb2")
+        wrap(W("w1"), ZHEAD, "p2", 0)
+        for j in range(3):
+            mm(PS("psa", j), MB(MA2), ch("p2", j), False, True)
+            act(ch("pq", j), PS("psa", j))
+        cp(L4, W("w1"))
+        mstep("ma", "mb", R("mb2"), L2, copy="ma2")
+        act(R("p3"), R("pq"), idx=L4)
+        for j in range(3):
+            mm(PS("psb", j), MB(MY), ch("pq", j), True, True)
+            mm(PS("psa", j), MB(MX2), ch("pq", j), True, False)
+            mm(PS("psa", j), MB(MOFF), ch("pq", j), False, False)
+        wrap(W("w0"), ZPTR, "p3", 0)
+        for j in range(3):
+            act(ch("yy", j), PS("psb", j), bias=YB)
+            mm(PS("psa", j), MB(MX3), ch("p3", j), False, True)
+        cp(L8, W("w0"))
+        mstep("mb", "ma", R("ma2"), L4, copy="mb2")
+        act(R("p4"), R("p3"), idx=L8)
+        for j in range(3):
+            tt(ch("ta", j), PS("psa", j), ch("yy", j), ALU.min)
+        wrap(W("w1"), ZPTR, "p4", 0)
+        for j in range(3):
+            act(ch("aa", j), ch("ta", j), bias=B3)
+            mm(PS("psa", j), MB(ME0), ch(p0, j), True, False)
+            mm(PS("psb", j), MB(MS4), ch("p4", j), True, False)
+        mstep("ma", "mb", R("mb2"), L8, copy="ma2")
+        cp(L16, W("w1"))
+        act(R("p5"), R("p4"), idx=L16)
+        for j in range(3):
+            tt(ch("tb", j), R("ta"), ch("aa", j), ALU.min, idx=third(L8, j))
+            act(ch("yy", j), ch("tb", j), bias=YB)
+            mm(PS("psa", j), MB(MY), ch("p5", j), False, False)
+            mm(PS("psb", j), MB(MS5), ch("p5", j), False, False)
+        mstep(m5, "ma", R("ma2"), L16)
+        dma("g", T.yw[:], T[m5][:], [R(m5)], [tag("yw")], add=rd == 1, lat=5000 + 3000 * rd)
+        for j in range(3):
+            tt(ch("ff", j), R("tb"), ch("yy", j), ALU.min, idx=third(L16, j))
+            mm(PS("psa", j), R("mh16", 0, 128), ch("ff", j), False, True)
+            mm(PS("psb", j), R("mh16", 128, 256), ch("ff", j), False, True)
+            act(ch("hi", j), PS("psa", j), func=AF.Abs)
+            act(ch("eq", j), ch("hi", j), func=AF.Relu, bias=1.0, scale=-1.0)
+        wrap(W("w0", 0), ZLOWA, "ff", 0)
+        wrap(W("w0", 1), ZLOWB, "ff", 0)
+        cp(R("wi", 0, 144), W("w0", 0, 144))
+        ts(R("wi", 144, 288), R("wi", 0, 144), 2047, None, ALU.bitwise_and)
+        ts(R("wi", 288, 432), R("wi", 0, 144), 11, None, ALU.logical_shift_right)
+        tt(R("wi", 432, 576), R("wi", 144, 288), R("wi", 288, 432), ALU.min)
+        tt(R("wi", 576, 648), R("wi", 432, 504), R("wi", 504, 576), ALU.min)
+        cp(LL, R("wi", 576, 648))
+        cut = 72 - CFG["vsv"][rd]
+        act(cols("vs", 0, cut), R(m5), func=AF.Sign, bias=-0.5, idx=sub(LL, 0, cut))
+        if cut < 72:
+            ts(cols("vs", cut, 72), R(m5), 0.0, 2.0, ALU.is_gt, ALU.mult, idx=sub(LL, cut, 72))
+        wrap(W("w1"), ZONE, "eq", 0)
+        for j in range(3):
+            tt(ch("pp", j), PS("psb", j), ch("eq", j), ALU.mult)
+        wrap(W("w0"), ZONE16, "pp", 0)
+        ts(F("cm"), W("w1"), 1.0, None, ALU.max)
+        ts(F("off"), W("w1"), 0.0, FAR, ALU.is_equal, ALU.mult)
+        op("v", lambda: g.vector.reciprocal(ap(F("rc")), ap(F("cm"))), [F("cm")], [F("rc")], t=190 + 432 * CYC)
+        if cut < 72:
+            mm(W("w1"), MB(DI), half(R("ind"), rd), True, False)
+        wrap(W("w1"), ZNEG, "vs", 0, start=cut == 72)
+        tt(F("pf"), W("w0"), F("rc"), ALU.mult)
+        cvt(LP, F("pf"))
+
+    def turned():
+        tt(F("t6"), W("w1"), F("off"), ALU.add)
+        ts(F("turn"), F("t6"), 0.0, None, ALU.is_lt)
+
+    walk(0)
+    ts(F("npf"), F("pf"), -1.0, -float(E), ALU.mult, ALU.add)
+    for k in range(2):
+        tt(half(F("q"), k), F("off"), half(F("mkn"), k), ALU.add)
+        tt(half(F("qm"), k), F("npf"), half(F("q"), k), ALU.add)
+    for k in range(2):
+        tt(half(F("u"), k), W("w1"), half(F("qm"), k), ALU.max)
+        tt(half(F("sl"), k), half(F("u"), k), half(F("slotm"), k), ALU.min)
+        ts(R("msgo", 72 * k, 72 * k + 72), half(F("sl"), k), -1.0, 0.25, ALU.mult, ALU.add)
+    send(R("msgi"), R("msgo"), "amsg")
+    NV = CFG["nv"]
+    for j in list(range(NV, 6)) + list(range(NV)):
+        act(ch("so", j), R("sow"), idx=third(R("msgo"), j))
+
+    def sops(j):
+        return PS("psa" if j - NV < 3 else "psb", (j - NV) % 3)
+    for j in range(NV, 6):
+        mm(sops(j), MB(DI), ch("so", j), True, True)
+    turned()
+    tt(F("t1"), F("turn"), F("dce"), ALU.mult)
+    for k in range(2):
+        tt(half(fl, k), F("turn"), half(F("mk"), k), ALU.mult)
+    tt(F("t2"), F("t1"), F("dump"), ALU.add)
+    ts(half(F("u"), 0), half(fl, 0), float(E), None, ALU.mult)
+    ts(half(F("u"), 1), half(fl, 1), float(V), None, ALU.mult)
+    cp(LE1, F("t2"))
+    for k in range(2):
+        tt(half(F("u2"), k), F("pf"), half(F("hs"), k), ALU.subtract)
+    tt(F("tl"), F("u"), F("slot"), ALU.add)
+    tt(F("base"), F("u2"), fl, ALU.mult)
+    tt(F("dS"), half(F("sl"), 0), half(F("sl"), 1), ALU.subtract)
+    tt(F("dT"), half(F("tl"), 1), half(F("tl"), 0), ALU.subtract)
+    tt(F("hs2"), F("hs"), F("base"), ALU.add)
+    tt(F("dH"), half(F("hs2"), 1), half(F("hs2"), 0), ALU.subtract)
+    for lo, hi in zip(CFG["sc"][:-1], CFG["sc"][1:]):
+        scatter("p0a", LE1, lo, hi)
+
+    arrive(R("nsw", 0, E), "aso")
+    arrive(R("nsw", E, E + V), "am0")
+    arrive(R("msgi"), "amsg")
+    for j in range(NV, 6):
+        act(ch("ng", j), R("nsw"), idx=third(R("msgi"), j))
+    for j in range(3):
+        act(ch("tab", j, E), R("p0a"), scale=GS, idx=third(LP, j))
+    for j in range(6):
+        if j < NV:
+            tt(ch("pr2", j), R("nsw"), ch("so", j), ALU.mult, idx=third(R("msgi"), j))
+        else:
+            tt(ch("pr2", j), sops(j), ch("ng", j), ALU.mult)
+    wrap(W("w0"), ZONE, "pr2", 0)
+    wrap(W("w1"), ZONE, "pr2", V)
+    cp(F("a0"), W("w0"))
+    tt(mask, W("w1"), F("a0"), ALU.is_gt)
+    tt(F("t0"), mask, F("dT"), ALU.mult)
+    tt(F("t2"), mask, F("dH"), ALU.mult)
+    tt(F("t3"), F("t0"), half(F("tl"), 0), ALU.add)
+    tt(F("t5"), F("t2"), half(F("hs2"), 0), ALU.add)
+    cp(LT, F("t3"))
+    tt(F("t1"), mask, F("dS"), ALU.mult)
+    tt(F("t4"), F("t1"), half(F("sl"), 0), ALU.subtract)
+    cvt(LC, F("t4"))
+    walk(1)
+    act(R("tab", E + V, 2 * E), R("p0b"), scale=GS, idx=LP)
+    tt(F("t8"), F("t7"), F("off"), ALU.add)
+    tt(F("t1"), W("w1"), F("t8"), ALU.max)
+    tt(F("t2"), F("t1"), F("dumpm"), ALU.min)
+    ts(LE2, F("t2"), 8192.0, None, ALU.add)
+    turned()
+    for k in range(2):
+        tt(half(F("u"), k), F("turn"), half(F("q"), k), ALU.mult)
+    tt(F("base"), F("u"), F("tl"), ALU.add)
+    cp(R("ylu"), F("base"))
+    scatter("p0b", LE2, 0, 72)
+
+    def rows_out(out, w, z, data, stage):
+        for j in range(16):
+            mm(W(w, 0, 144), zsel(z, j), R(data, 144 * j, 144 * j + 144), j == 0, j == 15)
+        act(stage, W(w, 0, 144))
+        dma("a", out[:], ap(stage), [stage], [tag(w + "out")], lat=2400)
+    for k in range(2):
+        act(R("yg", V * k, V * k + V), R("tab"), idx=R("ylu", 72 * k, 72 * k + 72))
+    rows_out(T.yl, "w0", ZEDGE, "yg", F("sl"))
+    lo = 0
+    for j in range(6):
+        ps = PS("psa" if j < 3 else "psb", j % 3)
+        mm(ps, MB(MSG), ch("ew", j), True, True)
+        tt(ch("yso", j), ps, ch("spb", j), ALU.mult)
+        if j in CFG["ysc"]:
+            dma("s", T.ys[:, CH * lo:CH * (j + 1)], T.yso[:, CH * lo:CH * (j + 1)],
+                [R("yso", CH * lo, CH * (j + 1))], [tag("ys", j)], lat=2200 + 400 * (j + 1 - lo))
+            lo = j + 1
+    rows_out(T.yh, "w1", ZH89, "ew", F("slotm"))
+
+    emit(g, T, schedule(ops), n_in, n_out)
+
+
+def meet(a, b):
+    return any(x[0] == y[0] and x[1] < y[2] and y[1] < x[2] for x in a for y in b)
+
+
+def clash(o, p):
+    return meet(o["rd"], p["wr"]) or meet(o["wr"], p["wr"]) or meet(o["wr"], p["rd"])
+
+
+ORDER = {}
+
+
+def schedule(ops):
+    n = len(ops)
+    if n in ORDER:
+        return [ops[i] for i in ORDER[n]]
+    pred = [[] for _ in ops]
+    succ = [[] for _ in ops]
+    by = {}
+    last = {}
+
+    def gap(j, i):
+        p, o = ops[j], ops[i]
+        if p["kind"] == "r":
+            return p["lat"] if o["kind"] == "x" else p["t"]
+        if p["kind"] == "d":
+            return p["lat"]
+        if p["kind"] == o["kind"] == "x":
+            return o["lat"]
+        return p["t"] + (0 if p["q"] == o["q"] == "p" else EST["wake"])
+    for i, o in enumerate(ops):
+        seen = set()
+        for x in o["rd"] + o["wr"]:
+            seen.update(by.get(x[0], ()))
+        ps = [j for j in sorted(seen) if clash(o, ops[j])]
+        for x in o["rd"] + o["wr"]:
+            by.setdefault(x[0], set()).add(i)
+        if o["kind"] == "r":
+            if "r" in last:
+                ps.append(last["r"])
+            last["r"] = last[o["sem"]] = i
+        if o["kind"] == "x":
+            ps.append(last[o["sem"]])
+            if "x" in last:
+                ps.append(last["x"])
+            o["lat"] = ops[last[o["sem"]]]["lat"] - 2000
+            last["x"] = i
+        for j in ps:
+            pred[i].append((j, gap(j, i)))
+            succ[j].append((i, gap(j, i)))
+    tail = [o["lat"] if o["kind"] == "d" else o["t"] for o in ops]
+
+    def place(order, forward):
+        start = [0.0] * n
+        busy = {q: [] for q in "vapgsx"}
+        for i in order:
+            d = ops[i]["t"]
+            if forward:
+                t = max([start[j] + w for j, w in pred[i]], default=0.0)
+            else:
+                t = max([start[j] + ops[j]["t"] + w - d for j, w in succ[i]] + [tail[i] - d])
+            b = busy[ops[i]["q"]]
+            at = len(b)
+            for k in range(len(b)):
+                s, e = b[k]
+                if e <= t:
+                    continue
+                if t + d <= s:
+                    at = k
+                    break
+                t = e
+            b.insert(at, (t, t + d))
+            start[i] = t
+        return start
+
+    state = [EST["seed"]]
+
+    def draw():
+        state[0] = (state[0] * 6364136223846793005 + 1442695040888963407) % (1 << 64)
+        return (state[0] >> 33) / float(1 << 31)
+    best, order = None, list(range(n))
+    for _ in range(EST["rounds"]):
+        for _ in range(2):
+            st = place(order, True)
+            end = max(st[i] + tail[i] for i in range(n))
+            if best is None or end <= best[0]:
+                best = (end, sorted(range(n), key=lambda i: (st[i], i)), st)
+            back = place(sorted(range(n), key=lambda i: (-(st[i] + ops[i]["t"]), -i)), False)
+            order = sorted(range(n), key=lambda i: (-(back[i] + ops[i]["t"]), i))
+        t0 = draw() * best[0]
+        key = [s + ((draw() + draw() + draw() - 1.5) * 2 * EST["sig"] if abs(s - t0) < EST["win"] else 0.0) for s in best[2]]
+        for i in range(n):
+            for j, w in pred[i]:
+                if key[i] <= key[j]:
+                    key[i] = key[j] + 1e-3
+        order = sorted(range(n), key=lambda i: key[i])
+    ORDER[n] = best[1]
+    ORDER["end"] = best[0]
+    return [ops[i] for i in best[1]]
+
+
+def emit(g, T, ops, n_in, n_out):
+    deps = []
+    by = {}
+    for i, o in enumerate(ops):
+        seen = set()
+        for x in o["rd"] + o["wr"]:
+            seen.update(by.get(x[0], ()))
+        d = {}
+        for j in sorted(seen, reverse=True):
+            p = ops[j]
+            key = p["q"] if p["kind"] == "c" else ("one", j)
+            if key in d or p["kind"] == "r" or o["kind"] == "x" or (o["q"] == "p" and p["q"] == "p"):
+                continue
+            if clash(o, p):
+                d[key] = j
+        deps.append(d)
+        for x in o["rd"] + o["wr"]:
+            by.setdefault(x[0], set()).add(i)
+    need = set()
+    known = {q: {} for q in "vapgs"}
+    clock = {}
+    waits = []
+    for i, o in enumerate(ops):
+        w = []
+        if o["kind"] != "x":
+            k = known[o["q"]]
+            for key, j in sorted(deps[i].items(), key=lambda t: -t[1]):
+                if k.get(key, -1) >= j:
+                    continue
+                w.append(j)
+                need.add(j)
+                k[key] = j
+                for kk, jj in clock[j].items():
+                    if k.get(kk, -1) < jj:
+                        k[kk] = jj
+            clock[i] = dict(k)
+        else:
+            clock[i] = {}
+        waits.append(w)
+    eng = {"v": g.vector, "a": g.scalar, "p": g.tensor, "g": g, "s": g.sync}
+    cnt = {q: 0 for q in "vapg"}
+    mark = {}
+    nd = 0
+    sent = 0
+    waited = {}
+    for i, o in enumerate(ops):
+        if o["kind"] == "x":
+            mark[i] = (o["sem"], n_in)
+            continue
+        for j in waits[i]:
+            eng[o["q"]].wait_ge(T.sem[mark[j][0]], mark[j][1])
+            waited[mark[j][0]] = max(waited.get(mark[j][0], 0), mark[j][1])
+        ins = o["fn"]()
+        if o["kind"] == "d":
+            mark[i] = ("d%d" % nd, 16)
+            ins.then_inc(T.sem["d%d" % nd], 16)
+            nd += 1
+        elif o["kind"] == "r":
+            sent += n_out
+        elif i in need:
+            cnt[o["q"]] += 1
+            mark[i] = ("c" + o["q"], cnt[o["q"]])
+            ins.then_inc(T.sem["c" + o["q"]], 1)
+    g.wait_ge(T.sem.lsent, sent)
+    for s, c in mark.values():
+        if waited.get(s, 0) < c:
+            g.wait_ge(T.sem[s], c)
+            waited[s] = c

@@ -3,41 +3,55 @@ from concourse.mybir import AluOpType as ALU, ActivationFunctionType as AF
 V = 1152
 E = 2304
 CH = 384
-BIG = 32768.0
-FAR = 1e6
+BIG = 16384.0
+FAR = 1048576.0
+MID = 576
+KNOTS = ((0, 8), (64, 4), (192, 2), (320, 1), (448, 1), (576, 1), (704, 1), (832, 2), (960, 4), (1088, 8), (1152, 0))
 BF, F32, F16, I32, U16 = "bfloat16", "float32", "float16", "int32", "uint16"
-EST = dict(cyc=1.04, gath=1.55, scat=3.8, pe=0.6, wake=100, link=80.0, rounds=250, sig=1500.0, win=4000.0, seed=1)
+EST = dict(cyc=0.9, gath=1.55, scat=3.8, pe=0.45, wake=100, link=70.0, rounds=1000, sig=1500.0, win=4000.0, seed=1)
 CFG = dict(
     ha=36,
     sc=(0, 12, 24, 36, 48, 60, 72),
-    nv=1,
-    xc=(0, 24, 52, 72),
-    vsv=(0, 30),
+    sc2=(0, 24, 72),
+    xc=(0, 8, 32, 56, 72),
+    lg=(0, 72),
+    pg=(0, 72),
+    pc=(0, 30, 52, 72),
+    m0=(72, 72),
+    p5=(0, 0),
+    eqa=((), ()),
+    vsv=(0, 0),
     ysc=(1, 3, 5),
 )
 
+
+def coded(v):
+    u = v - MID
+    return 8 * u - 4 * max(-512, min(512, u)) - 2 * max(-384, min(384, u)) - max(-256, min(256, u))
+
+
 SB = {
     "spb": (E, BF), "lvi": (144, I32), "lvu": (144, U16),
-    "hdi": (288, I32), "hdd": (576, I32), "hdb": (576, BF),
-    "et": (E, BF), "ct": (V, BF), "cc": (V, BF), "tab": (2 * E, BF), "ew": (E + V, BF),
+    "hdi": (144, I32), "hdd": (288, I32), "hdb": (432, BF), "hu": (576, F16),
+    "et": (E + V, BF), "ct": (V, BF), "cc": (V, BF), "tab": (2 * E, BF),
     "a16": (V, BF), "xo": (V, BF), "xn": (V, BF), "h192": (V, BF), "hi": (V, BF),
-    "pa16": (V, F16), "pb16": (V, F16), "sow": (E + V, BF), "nsw": (E + V, BF), "so": (E, BF), "ng": (E, BF), "pr2": (E, BF),
-    "p0a": (V, BF), "p0b": (V, BF), "p1": (V, BF), "p2": (V, BF), "pq": (V, BF), "p3": (V, BF), "p4": (V, BF), "p5": (V, BF),
+    "pa16": (V, F16), "pb16": (V, F16), "sow": (2 * E + 80, BF), "nsw": (E + 80, BF),
+    "no0": (V, BF), "ys1": (V, BF), "ng": (V, BF), "pr": (V, BF), "pr2": (V, BF),
+    "p0a": (V, BF), "p1": (V, BF), "p2": (V, BF), "q4": (V, BF), "p3": (V, BF), "q8": (V, BF), "p4": (V, BF),
+    "p5a": (V, BF), "p5b": (V, BF),
     "ma": (V, BF), "mb": (V, BF), "ma2": (V, BF), "mb2": (V, BF), "m5a": (V, BF), "m5b": (V, BF),
-    "yy": (V, F32), "ta": (V, F32), "tb": (V, F32), "aa": (V, F32), "ff": (V, F16),
-    "eq": (V, BF), "pp": (V, F16), "vs": (V, BF), "yg": (E, BF), "yso": (E, BF),
-    "lst": (72 * 12, U16), "msgo": (144, U16), "msgi": (144, U16), "ylu": (144, U16),
-    "wf": (72 * 64, F32), "wi": (72 * 10, I32), "ind": (144, BF),
-    "pi": (4, I32), "col": (64, F32), "oh": (16, F32), "jf": (144, F32), "jb": (128, BF), "b128": (18, F32),
-    "cb1": (18, F32), "cb2": (18, F32), "cb3": (18, F32), "dd": (128 * 5, BF),
-    "zb": (144 * 6, BF), "zh": (144 * 3, F16), "mb16": (128 * 17, BF), "mh16": (128 * 2, F16), "i16": (72, F32),
+    "eq": (V, BF), "pp": (V, BF), "vs": (V, BF), "yg": (E, BF), "yso": (E, BF),
+    "lst": (72 * 14, U16), "msgo": (72, U16), "msgi": (72, U16), "ylu": (144, U16),
+    "wf": (72 * 64, F32), "wb": (72 * 16, BF),
+    "pi": (4, I32), "col": (64, F32), "oh": (16, F32), "jf": (144, F32), "jb": (144, BF), "b128": (18, F32),
+    "cb1": (18, F32), "cb3": (18, F32), "dd": (128 * 3, BF),
+    "zb": (144 * 7, BF), "zh": (144, F16), "mb16": (128 * 24, BF), "mh16": (128 * 4, F16), "i16": (72, F32),
 }
 SCRATCH = {k: ("sbuf", [128, n], d) for k, (n, d) in SB.items()}
-SCRATCH.update({"psa": ("psum", [128, 1536], F32), "psb": ("psum", [128, 1536], F32),
-                "w0": ("psum", [128, 512], F32), "w1": ("psum", [128, 512], F32)})
-PSUM = ("psa", "psb", "w0", "w1")
+PSUM = ["k%d" % i for i in range(8)]
+SCRATCH.update({k: ("psum", [128, 512], F32) for k in PSUM})
 NDMA = 24
-SEMAPHORES = (["cv", "ca", "cp", "cg", "lsent", "ax0", "ax1", "ax2", "aso", "am0", "amsg"]
+SEMAPHORES = (["cv", "ca", "cp", "cg", "lsent", "ax0", "ax1", "ax2", "ax3", "am0", "amsg"]
               + ["d%d" % i for i in range(NDMA)])
 
 
@@ -53,24 +67,21 @@ def rank_program(g, core, T, topo):
     ops = []
     CYC = EST["cyc"]
 
-    def R(name, lo=0, hi=None, step=1, p=None):
-        return (name, lo, SB[name][0] if hi is None else hi, step, p)
+    def R(name, lo=0, hi=None, step=1):
+        return (name, lo, SB[name][0] if hi is None else hi, step)
 
     def sub(r, lo, hi):
-        return (r[0], r[1] + lo, r[1] + hi, 1, None)
+        return (r[0], r[1] + lo, r[1] + hi, 1)
 
     def tag(name, k=0):
-        return (name, k, k + 1, 1, None)
+        return (name, k, k + 1, 1)
 
     def ap(r):
-        name, lo, hi, step, p = r
-        ps = slice(None) if p is None else slice(*p)
-        return T[name][ps, lo:hi] if step == 1 else T[name][ps, lo:hi:step]
+        name, lo, hi, step = r
+        return T[name][:, lo:hi] if step == 1 else T[name][:, lo:hi:step]
 
     def span(r):
-        if r[0] in PSUM:
-            return (r[0], r[1] // 512 * 512, (r[2] + 511) // 512 * 512)
-        return r[:3]
+        return (r[0], 0, 512) if r[0] in PSUM else r[:3]
 
     def width(r):
         return (r[2] - r[1] + r[3] - 1) // r[3]
@@ -115,45 +126,47 @@ def rank_program(g, core, T, topo):
         op("v", lambda: g.vector.tensor_copy(ap(out), src(in_, idx)), aps(in_, idx), [out],
            t=cost(in_, 0.5 if two(out, in_) else 1, idx))
 
-    def cvt(out, in_):
-        ts(out, in_, 0.25, None, ALU.add)
+    def recip(out, in_):
+        op("v", lambda: g.vector.reciprocal(ap(out), ap(in_)), [in_], [out], t=190 + 6 * width(out) * CYC)
+
+    def fill(out, c):
+        op("v", lambda: g.vector.memset(ap(out), c), [], [out], t=64 * CYC)
 
     def act(out, in_, func=AF.Identity, bias=0.0, scale=1.0, idx=None):
         op("a", lambda: g.scalar.activation(ap(out), src(in_, idx), func, bias=sc(bias), scale=sc(scale)),
            aps(in_, bias, scale, idx), [out], t=cost(in_, 1, idx))
 
-    def mm(out, lhsT, rhs, start, stop):
-        op("p", lambda: g.tensor.matmul(ap(out), ap(lhsT), ap(rhs), start, stop), [lhsT, rhs], [out],
-           t=max(64, width(rhs)) * EST["pe"])
+    def mms(out, terms, start=True, stop=True):
+        k = len(terms) - 1
+        op("p", lambda: [g.tensor.matmul(ap(out), ap(l), ap(r), start and i == 0, stop and i == k)
+                         for i, (l, r) in enumerate(terms)][-1],
+           [(x[0], x[1], x[2], 1) for t in terms for x in t], [out], t=sum(max(64, width(r)) for l, r in terms) * EST["pe"])
 
-    def iota(out, pattern, base, cm, after=()):
+    def iota(out, pattern, base, cm):
         if SB[out[0]][1] == I32:
             f = lambda: g.iota(ap(out), pattern, base, cm)
         else:
             f = lambda: g.iota(ap(out), pattern, base, cm, allow_small_or_imprecise_dtypes=True)
-        op("g", f, list(after), [out], t=130 + 2 * width(out) * CYC)
+        op("g", f, [], [out], t=130 + 2 * width(out) * CYC)
 
     def gcopy(out, in_):
         op("g", lambda: g.affine_select(ap(out), ap(in_), [[0, in_[2] - in_[1]]], ALU.is_ge, 0.0, 0, 0), [in_], [out],
            t=170 + 2 * width(out) * CYC)
 
-    def dma(q, o, i, reads, writes, add=False, lat=2600):
+    def dma(q, o, i, reads, writes, add=False, lat=2400):
         eng = {"g": g, "s": g.sync, "a": g.scalar}[q]
         f = (lambda: eng.dma_start(o, i, accum_op=ALU.add)) if add else (lambda: eng.dma_start(o, i))
-        op(q, f, reads, writes, kind="d", t=400 if q == "g" else 100, lat=lat)
+        op(q, f, reads, writes, kind="d", t=900 if q == "g" else 100, lat=lat)
 
-    def send(dst, srcr, sem):
+    def send(dst, srcr, sem, nbytes=2):
         op("g", lambda: g.remote_dma(ap(dst), ap(srcr), T.sem[sem], T.sem.lsent, pid, rid, out_mask), [srcr], [], kind="r",
-           t=400, sem=sem, lat=2700 + width(srcr) * 256 / EST["link"])
+           t=400, sem=sem, lat=2700 + width(srcr) * 128 * nbytes / EST["link"])
 
     def arrive(dst, sem):
         op("x", None, [], [dst], kind="x", sem=sem, t=0)
 
-    def PS(name, j, w=CH):
-        return (name, 512 * j, 512 * j + w, 1, None)
-
-    def W(name, k=0, w=72):
-        return (name, 72 * k, 72 * k + w, 1, None)
+    def K(b, lo=0, hi=72):
+        return (PSUM[b], lo, hi, 1)
 
     def ch(name, j, base=0):
         return R(name, base + CH * j, base + CH * (j + 1))
@@ -161,192 +174,210 @@ def rank_program(g, core, T, topo):
     def cols(name, lo, hi, base=0):
         return R(name, base + 16 * lo, base + 16 * hi)
 
-    def third(lst, j):
-        return sub(lst, 24 * j, 24 * j + 24)
-
     def C(i):
         return R("col", i, i + 1)
 
     def OH(i):
         return R("oh", i, i + 1)
 
-    slots = {}
+    slots = {"wf": {}, "wb": {}, "col": {}, "mb16": {}, "zb": {}, "lst": {}}
+
+    def named(buf, name, w):
+        s = slots[buf]
+        if name not in s:
+            s[name] = sum(x[1] for x in s.values()), w
+        lo, w = s[name]
+        return R(buf, lo, lo + w)
 
     def F(name, w=1):
-        if name not in slots:
-            slots[name] = sum(x[1] for x in slots.values()), w
-        lo, w = slots[name]
-        return R("wf", 72 * lo, 72 * (lo + w))
+        return named("wf", name, 72 * w)
+
+    def B(name, w=1):
+        return named("wb", name, 72 * w)
+
+    def C(name):
+        return named("col", name, 1)
+
+    def M(name):
+        return named("mb16", name, 128)
+
+    def Z(name):
+        return named("zb", name, 144)
+
+    def L(name):
+        return named("lst", name, 72)
 
     def half(r, k):
         return sub(r, 72 * k, 72 * k + 72)
 
-    def MB(i):
-        return R("mb16", 128 * i, 128 * (i + 1))
+    def pairs(x):
+        return list(zip(x[:-1], x[1:]))
 
-    def ZR(z):
-        return R(z[0], z[1], z[1] + 144)
+    def wterms(z, data, base, lo, hi):
+        return [((z[0], z[1] + 15 - i, z[1] + 143 - i, 1), R(data, base + 16 * lo + i, base + 16 * hi, 16)) for i in range(16)]
 
-    def zsel(z, i):
-        return (z[0], z[1] + 15 - i, z[1] + 143 - i, 1, None)
-
-    def wrap(out, z, data, base, start=True, stop=True):
-        for i in range(16):
-            mm(out, zsel(z, i), R(data, base + i, base + V, 16), start and i == 0, stop and i == 15)
+    def wrap(b, z, data, base=0, lo=0, hi=72, start=True, stop=True):
+        mms(K(b, lo, hi), wterms(z, data, base, lo, hi), start, stop)
 
     PARTS = ((0, CFG["ha"]), (CFG["ha"], 72))
-    ZONE, ZHEAD, ZEDGE, ZPTR, ZNEG, ZH89 = [("zb", 144 * i) for i in range(6)]
-    ZONE16, ZLOWA, ZLOWB = [("zh", 144 * i) for i in range(3)]
-    (PF, RF, C15, HV, TV, EV, LOWA, LOWB, A2, D13, GS, YB, B3, LT12, LT8, LT6, P1C, NTV, W67, R1, RH, TA, WA, OFF,
-     T0, T1, T2, T3, T4, T5, T6, T7, T8) = [C(i) for i in range(33)]
-    (DNI, DI, D16, D15, MA1A, MA1B, MA2, MX2, MX3, MOFF, MY, ME0, MS4, MS5, MSG, MT1, MT2) = range(17)
-    DD, DN, DM, D8N, D8 = [R("dd", 128 * i, 128 * i + 128) for i in range(5)]
-    for nm in ("slot", "slotm", "hs", "hs2", "fl", "mk", "q", "qm", "u", "u2", "sl", "tl", "base", "mkn"):
-        F(nm, 2)
-    LT, LC, L1, L2, L4, L8, L16, LL, LP, LE1, LE2 = [R("lst", 72 * i, 72 * i + 72) for i in range(11)]
-    mask, fl = half(F("mk"), 1), F("fl")
+    THIRDS = ((0, 24), (24, 48), (48, 72))
+    A, Bk, W0, W1 = (0, 1, 2), (3, 4, 5), 6, 7
+    PF, RF, C15 = C("pf"), C("rf"), C("c15")
+    DD, DN, DM = [R("dd", 128 * i, 128 * i + 128) for i in range(3)]
+    JB = R("jb", 0, 128)
+    slot0, slot1 = half(F("slot", 2), 0), half(F("slot"), 1)
+    M0 = E + V + 80
+    maskb, nmask = R("sow", E + V, E + V + 72), R("nsw", V, V + 72)
 
     sp0 = R("spb")
-    dma("s", T.spb[:], T.sp[:], [], [sp0], lat=4800)
-    dma("a", T.hdi[0:64, :], T.hd[:], [], [R("hdi")])
-    dma("a", T.lvi[:], T.lv[:], [], [R("lvi")])
+    dma("s", T.lvi[:], T.lv[:], [], [R("lvi")], lat=2300)
+    dma("a", T.hdi[:], T.hd[:], [], [R("hdi")], lat=2300)
+    dma("s", T.spb[:], T.sp[:], [], [sp0], lat=4400)
+    ops[2]["after"] = [0, 1]
 
     iota(R("pi", 0, 1), [[0, 1]], 0, 1)
     iota(R("jf"), [[1, 144]], 0, 0)
+    iota(R("jb"), [[1, 144]], 0, 0)
     iota(R("b128"), [[128, 18]], 0, 0)
-    iota(R("jb"), [[1, 128]], 0, 0)
     iota(R("i16"), [[16, 72]], 0, 0)
     ts(R("pi", 1, 2), R("pi", 0, 1), 15, None, ALU.bitwise_and)
     cp(PF, R("pi", 0, 1))
-    ts(R("pi", 2, 3), R("pi", 0, 1), 1, None, ALU.bitwise_and)
     cp(RF, R("pi", 1, 2))
-    ts(R("pi", 3, 4), R("pi", 1, 2), 1, None, ALU.logical_shift_right)
     ts(R("oh"), R("jf", 0, 16), RF, None, ALU.is_equal)
     ts(C15, PF, RF, 15.0, ALU.subtract, ALU.add)
-    ts(HV, RF, 4.0, 0.5, ALU.is_lt, ALU.mult)
-    ts(T0, OH(4), OH(8), OH(9), ALU.add, ALU.add)
-    act(A2, OH(2), bias=OH(0), scale=-1.0)
-    act(D13, OH(3), bias=OH(1), scale=-1.0)
-    ts(R("cb3"), R("b128"), OH(9), OH(4), ALU.mult, ALU.subtract)
-    ts(R("cb1"), R("b128"), OH(6), T0, ALU.mult, ALU.add)
-    ts(TV, RF, 2.0, HV, ALU.is_lt, ALU.subtract)
-    act(R("cb2"), R("b128"), scale=D13)
+
+    def rows(name, base, *terms):
+        at = base
+        for k, (r, w) in enumerate(terms):
+            out = C(name) if k == len(terms) - 1 else C(name + str(k))
+            act(out, OH(r), bias=at, scale=float(w))
+            at = out
+        return C(name)
+    ts(C("k0a"), RF, 4.0, 2048.0 - BIG, ALU.is_lt, ALU.mult)
+    act(C("k0b"), OH(11), bias=BIG, scale=1.0 - BIG)
+    act(C("k0"), C("k0a"), bias=C("k0b"))
+    act(C("set"), OH(0), scale=16.0)
+    ts(R("cb1"), R("b128"), OH(1), C("k0"), ALU.mult, ALU.add)
     for b in range(9):
-        act(R("et", 128 * b, 128 * b + 128), R("jb"), bias=R("cb1", b, b + 1), scale=OH(5))
+        act(R("et", 128 * b, 128 * b + 128), JB, bias=R("cb1", b, b + 1), scale=C("set"))
     for b in range(9, 18):
-        ts(R("et", 128 * b, 128 * b + 128), R("jb"), OH(5), R("cb1", b, b + 1), ALU.mult, ALU.add)
-    cp(R1, R("pi", 2, 3))
-    cp(RH, R("pi", 3, 4))
-    ts(DD, R("jb"), C15, 15.0, ALU.subtract, ALU.add)
-    ts(LT12, RF, 12.0, None, ALU.is_lt)
-    ts(LT8, RF, 8.0, None, ALU.is_lt)
-    ts(LT6, RF, 6.0, None, ALU.is_lt)
-    ts(DN, DD, 0.0, 200.0, ALU.is_lt, ALU.mult)
-    hp = (0, 64)
-    ts(R("hdd", 0, 288, 1, hp), R("hdi", 0, 288, 1, hp), 127, None, ALU.bitwise_and)
-    ts(R("hdd", 288, 576, 1, hp), R("hdi", 0, 288, 1, hp), 0xF80, None, ALU.bitwise_and)
+        ts(R("et", 128 * b, 128 * b + 128), JB, C("set"), R("cb1", b, b + 1), ALU.mult, ALU.add)
+    for i, w in enumerate((8.0, -4.0, -2.0, -1.0)):
+        ts(R("mh16", 128 * i, 128 * i + 128), JB, PF, w, ALU.is_equal, ALU.mult)
     cp(R("lvu"), R("lvi"))
-    cp(R("hdb", 0, 576, 1, hp), R("hdd", 0, 576, 1, hp))
-    for r in range(4):
-        dma("s", T.et[r::16, :], T.hdb[0:64, 288 * (r % 2):288 * (r % 2) + 288], [R("hdb"), R("et")], [tag("etrow", r)])
-    etrows = [tag("etrow", r) for r in range(4)]
-    for i, w in ((DNI, -1.0), (DI, 1.0), (D16, 16.0), (D15, -15.9375)):
-        ts(MB(i), R("jb"), PF, w, ALU.is_equal, ALU.mult)
+    ts(R("hu", 0, 144), R("hdi"), float(MID), None, ALU.subtract)
+    ts(R("hdd", 0, 144), R("hdi"), 127, None, ALU.bitwise_and)
+    ts(R("hdd", 144, 288), R("hdi"), 0xF80, None, ALU.bitwise_and)
+    for i, w in enumerate((512.0, 384.0, 256.0)):
+        ts(R("hu", 144 * i + 144, 144 * i + 288), R("hu", 0, 144), w, -w, ALU.min, ALU.max)
+    mms(K(W0, 0, 144), [(R("mh16", 128 * i, 128 * i + 128), R("hu", 144 * i, 144 * i + 144)) for i in range(4)])
+    act(R("hdb", 288, 432), K(W0, 0, 144))
+    cp(R("hdb", 0, 288), R("hdd"))
+    for r, k in ((9, 0), (10, 1), (4, 2), (8, 2)):
+        dma("s", T.et[r::16, 0:E], T.hdb[:, 144 * k:144 * k + 144], [R("hdb", 144 * k, 144 * k + 144), R("et", 0, E)], [tag("etrow", r)])
+    etrows = [tag("etrow", r) for r in (9, 10, 4, 8)]
+    for nm, w in (("-1", -1.0), ("1", 1.0), ("-255/256", -0.99609375), ("-15/16", -0.9375), ("1/8", 0.125), ("1/4", 0.25), ("1/2", 0.5)):
+        ts(M(nm), JB, PF, w, ALU.is_equal, ALU.mult)
+    rows("t47", OH(4), (7, 1))
+    for s in (2, 4, 8):
+        act(C("t47x%d" % s), C("t47"), scale=float(s))
+    for (lo, s), (hi, _) in pairs(KNOTS):
+        act(C("ctb%d" % lo), C("t47"), bias=BIG, scale=coded(lo) - BIG)
+        act(R("ct", lo, hi), R("jb", 0, hi - lo), bias=C("ctb%d" % lo), scale=C("t47x%d" % s if s > 1 else "t47"))
+    act(C("scc"), OH(2), scale=1 / 2048.0)
+    act(C("s3"), OH(3), scale=1 / 2048.0)
+    ts(R("cb3"), R("b128"), C("s3"), OH(11), ALU.mult, ALU.subtract)
     for b in range(9):
-        act(R("ct", 128 * b, 128 * b + 128), R("jb"), bias=R("cb2", b, b + 1), scale=A2)
-    for b in range(9):
-        act(R("cc", 128 * b, 128 * b + 128), R("jb"), bias=R("cb3", b, b + 1), scale=OH(8))
-    ts(ZR(ZHEAD), R("jf"), C15, HV, ALU.is_equal, ALU.mult)
-    ts(ZR(ZONE16), R("jf"), C15, None, ALU.is_equal)
-    act(half(F("slot"), 0), R("i16"), bias=RF)
-    act(half(F("slot"), 1), half(F("slot"), 0), bias=float(V))
-    act(F("dump"), half(F("slot"), 0), bias=float(E))
-    act(F("dump2"), half(F("slot"), 0), bias=float(E + V))
-    act(F("dumpm"), half(F("slot"), 0), bias=float(E - 8192))
-    act(F("slotm"), F("slot"), scale=-1.0)
+        act(R("cc", 128 * b, 128 * b + 128), JB, bias=R("cb3", b, b + 1), scale=C("scc"))
+    act(slot0, R("i16"), bias=RF)
+    act(slot1, slot0, bias=float(V))
+    act(F("dumpk"), slot0, bias=4096.0 - E, scale=-1.0)
+    act(F("keepk"), slot0, bias=4096.0 - V - 80, scale=-1.0)
+    ts(DD, JB, C15, 15.0, ALU.subtract, ALU.add)
+    ts(DN, DD, 0.0, 200.0, ALU.is_lt, ALU.mult)
     tt(DM, DD, DN, ALU.add)
-    act(EV, OH(5), bias=OH(6))
-    act(TA, OH(8), bias=R1, scale=8.0)
-    act(WA, TV, bias=OH(8))
-    act(T2, R1, bias=2.0)
-    act(T3, R1, bias=4.0)
-    act(T4, R1, bias=6.0)
-    act(W67, OH(6), bias=OH(7))
-    act(T5, RH, bias=4.0)
-    act(T6, RH, bias=12.0)
-    act(T7, RH, bias=13.0)
-    act(OFF, OH(8), scale=2048.0)
-    act(YB, LT12, scale=BIG)
-    act(B3, LT8, bias=YB, scale=-(BIG + 2048.0))
-    act(NTV, TV, scale=-1.0)
-    act(P1C, PF, bias=1.0)
-    act(LOWA, OH(13), bias=OH(12), scale=2048.0)
-    act(LOWB, OH(15), bias=OH(14), scale=2048.0)
-    act(T8, OH(8), bias=OH(9))
-    ts(T1, OH(2), OH(3), OH(4), ALU.add, ALU.add)
-    act(GS, T1, bias=1.0, scale=-2.0)
-    ts(D8N, DM, 8.0, -8.0, ALU.is_ge, ALU.mult)
-    tt(D8, DM, D8N, ALU.add)
-    for z, w in ((ZEDGE, EV), (ZPTR, W67), (ZLOWA, LOWA), (ZLOWB, LOWB), (ZNEG, -4096.0), (ZH89, T8), (ZONE, 1.0)):
-        ts(ZR(z), R("jf"), C15, w, ALU.is_equal, ALU.mult)
-    for m, d, at, w in ((MT1, DM, T3, TV), (MT2, DM, T4, HV), (MA1A, DM, TA, WA), (MA1B, DM, T2, HV), (MY, DM, T6, LT8),
-                        (MX2, D8, RH, LT8), (MX3, D8, T5, LT8), (MS4, DM, 0.0, W67), (MS5, DM, T7, LT6)):
-        ts(MB(m), d, at, w, ALU.is_equal, ALU.mult)
-    tt(MB(MA2), MB(MT1), MB(MT2), ALU.add)
-    for m, below, w in ((MOFF, 8.0, OFF), (ME0, 16.0, NTV), (MSG, 16.0, OH(4))):
-        ts(MB(m), DM, below, w, ALU.is_lt, ALU.mult)
-    ts(R("mh16", 0, 128), R("jb"), PF, LT12, ALU.is_equal, ALU.mult)
-    ts(R("mh16", 128, 256), R("jb"), P1C, LT12, ALU.is_equal, ALU.mult)
+    ts(R("zh"), R("jb"), C15, None, ALU.is_equal)
+    rows("w910", OH(9), (10, 1))
+    rows("w23", OH(2), (3, 1))
+    rows("wedge", OH(1), (0, 0.0625), (2, -1.0625))
+    act(C("wh0"), C("w910"), bias=C("w23"))
+    rows("wh", C("wh0"), (12, -0.25))
+    for z, w in (("head", C("w910")), ("edge", C("wedge")), ("min", OH(4)), ("one", 1.0), ("vote", 4096.0), ("neg", -1.0),
+                 ("h", C("wh"))):
+        ts(Z(z), R("jb"), C15, w, ALU.is_equal, ALU.mult)
+    rows("w78", OH(7), (8, 1))
+    act(C("at4"), C("w78"), bias=RF, scale=-2.0)
+    act(C("w4"), C("w78"), bias=OH(4))
+    act(C("r5"), RF, bias=-5.0)
+    rows("at8", C("r5"), (4, 5))
+    ts(C("w8a"), RF, 4.0, None, ALU.is_ge)
+    ts(C("lt9"), RF, 9.0, None, ALU.is_lt)
+    act(C("w8"), C("w8a"), scale=C("lt9"))
+    rows("th8", 0.0, (13, 16), (14, 5))
+    rows("th4", C("th8"), (12, 4), (14, 2))
+    rows("bw8", OH(13), (14, -1))
+    act(C("bw4"), C("bw8"), bias=OH(12))
+    ts(C("ord"), RF, 4.0, -1.0, ALU.is_gt, ALU.mult)
+    act(C("ord0"), C("ord"), bias=RF)
+    for k in (1, 8, 9):
+        act(C("ord%d" % k), C("ord0"), bias=float(k))
+    rows("pw", C("lt9"), (4, -1))
+    rows("pwb", C("pw"), (8, -1))
+    rows("atr", RF, (7, 1), (8, -1))
+    act(C("wr0"), C("w910"), bias=1.0, scale=-1.0)
+    rows("wr", C("wr0"), (11, -2))
+    act(C("atc"), RF, bias=7.0)
+    act(C("wc"), C("w23"), scale=2048.0)
+    act(C("n7"), OH(7), scale=-1.0)
+    for m, at, w in (("q4a", C("at4"), C("w4")), ("q8a", C("at8"), C("w8")), ("ea", C("ord0"), C("pw")), ("eb", C("ord8"), C("pw")),
+                     ("pa", C("ord1"), C("pw")), ("pb", C("ord9"), C("pwb")), ("p4", 0.0, OH(8)), ("rev", C("atr"), C("wr")),
+                     ("revc", C("atc"), C("wc"))):
+        ts(M(m), DM, at, w, ALU.is_equal, ALU.mult)
+    for m, below, w in (("q4b", C("th4"), C("bw4")), ("q8b", C("th8"), C("bw8")), ("ev", 16.0, C("n7")), ("sg", 16.0, OH(11))):
+        ts(M(m), DM, below, w, ALU.is_lt, ALU.mult)
+    tt(M("q4"), M("q4a"), M("q4b"), ALU.add)
+    tt(M("q8"), M("q8a"), M("q8b"), ALU.add)
+    fill(B("eps"), 2.0 ** -12)
     for rd in range(2):
         if CFG["vsv"][rd]:
-            ts(half(R("ind"), rd), R("jf", 0, 72), 72.0 - CFG["vsv"][rd], 65536.0, ALU.is_ge, ALU.mult)
+            ts(B("ind%d" % rd), R("jb", 0, 72), 72.0 - CFG["vsv"][rd], -65536.0, ALU.is_ge, ALU.mult)
 
-    XC = list(zip(CFG["xc"][:-1], CFG["xc"][1:]))
+    XC = pairs(CFG["xc"])
     for j, (lo, hi) in enumerate(XC):
         act(cols("a16", lo, hi), sp0, scale=16.0, idx=R("lvu", 72 + lo, 72 + hi))
         tt(cols("xo", lo, hi), sp0, cols("a16", lo, hi), ALU.add, idx=R("lvu", lo, hi))
         send(cols("xn", lo, hi), cols("xo", lo, hi), "ax%d" % j)
 
-    def xps(name, j):
-        return PS(name, j, 16 * (XC[j][1] - XC[j][0]))
+    def xk(banks, j):
+        b = at = 0
+        for lo, hi in XC[:j + 1]:
+            if at + 16 * (hi - lo) > 512:
+                b, at = b + 1, 0
+            at += 16 * (hi - lo)
+        return K(banks[b], at - 16 * (hi - lo), at)
     for j, (lo, hi) in enumerate(XC):
-        mm(xps("psa", j), MB(DNI), cols("xo", lo, hi), True, False)
-        mm(xps("psa", j), MB(DI), cols("a16", lo, hi), False, True)
-        mm(xps("psb", j), MB(D16), cols("xo", lo, hi), True, False)
-        mm(xps("psb", j), MB(D15), cols("a16", lo, hi), False, True)
+        mms(xk(A, j), [(M("-1"), cols("xo", lo, hi)), (M("1"), cols("a16", lo, hi))])
+        mms(xk(Bk, j), [(M("1"), cols("xo", lo, hi)), (M("-255/256"), cols("a16", lo, hi))])
     act(R("sow", V, E), R("a16"), scale=0.0625)
     for j, (lo, hi) in enumerate(XC):
-        act(cols("sow", lo, hi), xps("psa", j), scale=-1.0)
+        act(cols("sow", lo, hi), xk(A, j), scale=-1.0)
     for k in range(2):
         for lo, hi in PARTS:
-            tt(cols("tab", lo, hi, V * k), R("et"), cols("ct", lo, hi), ALU.add, idx=R("lvu", 72 * k + lo, 72 * k + hi), extra=etrows)
-        wrap(W("w0", k), ZHEAD, "tab", V * k)
-    iota(R("ew", 0, 768), [[0, 768]], 1, 0, after=[R("xo")])
-    send(R("nsw", 0, E), R("sow", 0, E), "aso")
-    iota(R("ew", 768, E + V), [[0, E + V - 768]], 1, 0, after=[R("sow", 0, E), R("ew", 0, 768)])
-    for r in range(2):
-        dma("s", T.ew[8 + r::16, 0:E], T.hdb[0:64, 288 * r:288 * r + 288], [R("hdb")], [R("ew")])
+            tt(cols("tab", lo, hi, V * k), R("et", 0, E), cols("ct", lo, hi), ALU.min, idx=R("lvu", 72 * k + lo, 72 * k + hi), extra=etrows)
 
     for j, (lo, hi) in enumerate(XC):
         arrive(cols("xn", lo, hi), "ax%d" % j)
     for j, (lo, hi) in enumerate(XC):
-        act(cols("h192", lo, hi), cols("xn", lo, hi), bias=192.0, scale=0.0625)
-        act(cols("hi", lo, hi), cols("h192", lo, hi), bias=-192.0)
-        tt(cols("pa16", lo, hi), xps("psa", j), cols("xn", lo, hi), ALU.mult)
-        tt(cols("pb16", lo, hi), xps("psb", j), cols("hi", lo, hi), ALU.mult)
-    wrap(W("w1"), ZONE16, "pa16", 0, True, False)
-    wrap(W("w1"), ZONE16, "pb16", 0, False, True)
-    cp(F("hs"), W("w0", 0, 144))
-    tt(F("dH"), half(F("hs"), 1), half(F("hs"), 0), ALU.subtract)
-    ts(F("t0"), W("w1"), 0.0, float(V), ALU.is_gt, ALU.mult)
-    ts(mask, W("w1"), 0.0, None, ALU.is_gt)
-    tt(F("t3"), F("t0"), half(F("slot"), 0), ALU.add)
-    tt(F("t2"), mask, F("dH"), ALU.mult)
-    cp(LT, F("t3"))
-    tt(F("t5"), F("t2"), half(F("hs"), 0), ALU.add)
-
-    def scatter(p0, le, lo, hi):
-        tt(R("ew"), cols(p0, lo, hi), cols("cc", lo, hi), ALU.mult, oidx=sub(le, lo, hi))
+        tt(cols("pa16", lo, hi), xk(A, j), cols("xn", lo, hi), ALU.mult)
+        ts(cols("hi", lo, hi), cols("xn", lo, hi), 1.5 * 2 ** 27, 1.5 * 2 ** 27, ALU.add, ALU.subtract)
+        tt(cols("pb16", lo, hi), xk(Bk, j), cols("hi", lo, hi), ALU.mult)
+    wrap(W1, R("zh"), "pa16", stop=False)
+    wrap(W1, R("zh"), "pb16", start=False)
+    ts(F("t0"), K(W1), 0.0, float(V), ALU.is_gt, ALU.mult)
+    tt(F("lt1"), F("t0"), slot0, ALU.add)
+    cp(L("t"), F("lt1"))
+    act(maskb, F("t0"), scale=1.0 / V)
+    fill(R("sow", E + V + 72, M0), 0.0)
 
     def mstep(out, win, dup, idx, o=ALU.add, copy=None):
         for lo, hi in PARTS:
@@ -354,201 +385,193 @@ def rank_program(g, core, T, topo):
             if copy:
                 gcopy(cols(copy, lo, hi), cols(out, lo, hi))
 
-    def walk(rd):
-        p0, m5 = ("p0a", "m5a") if rd == 0 else ("p0b", "m5b")
-        act(R(p0), R("tab", 0, E + V * rd), idx=LT)
-        cvt(L1, F("t5"))
-        act(R("p1"), R(p0), idx=L1)
-        wrap(W("w1"), ZEDGE, p0, 0)
-        if rd == 0:
-            cp(R("ma"), R("sow", 0, E), idx=LT)
-            ts(R("sow", E, E + V), R("ma"), -1.0, None, ALU.mult)
-            send(R("nsw", E, E + V), R("sow", E, E + V), "am0")
-        else:
-            for lo, hi in PARTS:
-                cp(cols("ma", lo, hi), R("sow"), idx=sub(LC, lo, hi))
-                gcopy(cols("ma2", lo, hi), cols("ma", lo, hi))
-        wrap(W("w0"), ZHEAD, "p1", 0)
-        tt(F("dce"), W("w1"), F("dump"), ALU.subtract)
-        ts(half(F("mk"), 0), mask, -1.0, 1.0, ALU.mult, ALU.add)
-        if rd == 0:
-            ts(F("mkn"), F("mk"), -FAR, FAR, ALU.mult, ALU.add)
-        else:
-            for h in range(2):
-                tt(half(F("u2"), h), F("dump2"), half(F("tl"), h), ALU.subtract)
-            tt(F("q"), F("u2"), F("mk"), ALU.mult)
-            tt(F("t7"), F("dce"), F("dumpm"), ALU.add)
-        cp(L2, W("w0"))
-        for j in range(3):
-            mm(PS("psa", j), MB(MA1A), ch("p1", j), True, False)
-            mm(PS("psa", j), MB(MA1B), ch("p1", j), False, False)
-        act(R("p2"), R("p1"), idx=L2)
-        if rd == 0:
-            mstep("mb", "ma", R("sow", E, E + V), L1, o=ALU.subtract, copy="mb2")
-        else:
-            mstep("mb", "ma", R("ma2"), L1, copy="mb2")
-        wrap(W("w1"), ZHEAD, "p2", 0)
-        for j in range(3):
-            mm(PS("psa", j), MB(MA2), ch("p2", j), False, True)
-            act(ch("pq", j), PS("psa", j))
-        cp(L4, W("w1"))
-        mstep("ma", "mb", R("mb2"), L2, copy="ma2")
-        act(R("p3"), R("pq"), idx=L4)
-        for j in range(3):
-            mm(PS("psb", j), MB(MY), ch("pq", j), True, True)
-            mm(PS("psa", j), MB(MX2), ch("pq", j), True, False)
-            mm(PS("psa", j), MB(MOFF), ch("pq", j), False, False)
-        wrap(W("w0"), ZPTR, "p3", 0)
-        for j in range(3):
-            act(ch("yy", j), PS("psb", j), bias=YB)
-            mm(PS("psa", j), MB(MX3), ch("p3", j), False, True)
-        cp(L8, W("w0"))
-        mstep("mb", "ma", R("ma2"), L4, copy="mb2")
-        act(R("p4"), R("p3"), idx=L8)
-        for j in range(3):
-            tt(ch("ta", j), PS("psa", j), ch("yy", j), ALU.min)
-        wrap(W("w1"), ZPTR, "p4", 0)
-        for j in range(3):
-            act(ch("aa", j), ch("ta", j), bias=B3)
-            mm(PS("psa", j), MB(ME0), ch(p0, j), True, False)
-            mm(PS("psb", j), MB(MS4), ch("p4", j), True, False)
-        mstep("ma", "mb", R("mb2"), L8, copy="ma2")
-        cp(L16, W("w1"))
-        act(R("p5"), R("p4"), idx=L16)
-        for j in range(3):
-            tt(ch("tb", j), R("ta"), ch("aa", j), ALU.min, idx=third(L8, j))
-            act(ch("yy", j), ch("tb", j), bias=YB)
-            mm(PS("psa", j), MB(MY), ch("p5", j), False, False)
-            mm(PS("psb", j), MB(MS5), ch("p5", j), False, False)
-        mstep(m5, "ma", R("ma2"), L16)
-        dma("g", T.yw[:], T[m5][:], [R(m5)], [tag("yw")], add=rd == 1, lat=5000 + 3000 * rd)
-        for j in range(3):
-            tt(ch("ff", j), R("tb"), ch("yy", j), ALU.min, idx=third(L16, j))
-            mm(PS("psa", j), R("mh16", 0, 128), ch("ff", j), False, True)
-            mm(PS("psb", j), R("mh16", 128, 256), ch("ff", j), False, True)
-            act(ch("hi", j), PS("psa", j), func=AF.Abs)
-            act(ch("eq", j), ch("hi", j), func=AF.Relu, bias=1.0, scale=-1.0)
-        wrap(W("w0", 0), ZLOWA, "ff", 0)
-        wrap(W("w0", 1), ZLOWB, "ff", 0)
-        cp(R("wi", 0, 144), W("w0", 0, 144))
-        ts(R("wi", 144, 288), R("wi", 0, 144), 2047, None, ALU.bitwise_and)
-        ts(R("wi", 288, 432), R("wi", 0, 144), 11, None, ALU.logical_shift_right)
-        tt(R("wi", 432, 576), R("wi", 144, 288), R("wi", 288, 432), ALU.min)
-        tt(R("wi", 576, 648), R("wi", 432, 504), R("wi", 504, 576), ALU.min)
-        cp(LL, R("wi", 576, 648))
-        cut = 72 - CFG["vsv"][rd]
-        act(cols("vs", 0, cut), R(m5), func=AF.Sign, bias=-0.5, idx=sub(LL, 0, cut))
-        if cut < 72:
-            ts(cols("vs", cut, 72), R(m5), 0.0, 2.0, ALU.is_gt, ALU.mult, idx=sub(LL, cut, 72))
-        wrap(W("w1"), ZONE, "eq", 0)
-        for j in range(3):
-            tt(ch("pp", j), PS("psb", j), ch("eq", j), ALU.mult)
-        wrap(W("w0"), ZONE16, "pp", 0)
-        ts(F("cm"), W("w1"), 1.0, None, ALU.max)
-        ts(F("off"), W("w1"), 0.0, FAR, ALU.is_equal, ALU.mult)
-        op("v", lambda: g.vector.reciprocal(ap(F("rc")), ap(F("cm"))), [F("cm")], [F("rc")], t=190 + 432 * CYC)
-        if cut < 72:
-            mm(W("w1"), MB(DI), half(R("ind"), rd), True, False)
-        wrap(W("w1"), ZNEG, "vs", 0, start=cut == 72)
-        tt(F("pf"), W("w0"), F("rc"), ALU.mult)
-        cvt(LP, F("pf"))
+    def hop(out, win, idx, lst=None, base=0, parts=PARTS):
+        for k, (lo, hi) in enumerate(parts):
+            act(cols(out, lo, hi, base), win, idx=sub(idx, lo, hi))
+            if lst:
+                wrap((W0, W1)[k], Z("head"), out, base, lo, hi)
+                cp(sub(lst, lo, hi), K((W0, W1)[k], lo, hi))
 
-    def turned():
-        tt(F("t6"), W("w1"), F("off"), ALU.add)
-        ts(F("turn"), F("t6"), 0.0, None, ALU.is_lt)
+    def merge(out, m, before, shifted):
+        for j in range(3):
+            mms(K(A[j], 0, CH), [(m, ch(before, j))])
+            tt(ch(out, j), K(A[j], 0, CH), ch(shifted, j), ALU.min)
+
+    def decode(b, x, lo, hi):
+        for k, w in enumerate((1024.0, 512.0, 256.0)):
+            ts(sub(half(x, k + 1), lo, hi), sub(x, lo, hi), w, -w, ALU.min, ALU.max)
+        mms(K(b, lo, hi), [(M(w), sub(half(x, k), lo, hi)) for k, w in enumerate(("1/8", "1/8", "1/4", "1/2"))])
+
+    def walk(rd):
+        p0, b0, m5 = ("p0a", 0, "m5a") if rd == 0 else ("tab", E + V, "m5b")
+        m0, c0 = ("sow", M0) if rd == 0 else ("ma", 0)
+        win = E + V * rd
+        hop(p0, R("tab", 0, win), L("t"), L("1"), b0)
+        mv = CFG["m0"][rd]
+        for lo, hi in PARTS:
+            for l, h, eng in ((lo, min(hi, mv), cp), (max(lo, mv), hi, act)):
+                if l < h:
+                    eng(cols(m0, l, h, c0), R("sow", 0, win), idx=sub(L("t"), l, h))
+            if rd == 0:
+                ts(cols("sow", lo, hi, E), cols(m0, lo, hi, c0), -1.0, None, ALU.mult)
+            else:
+                gcopy(cols("ma2", lo, hi), cols("ma", lo, hi))
+        if rd == 0:
+            send(R("nsw"), R("sow", E, 2 * E + 80), "am0")
+        hop("p1", R(p0, b0, b0 + V), L("1"), L("2"))
+        wrap(Bk[0], Z("edge"), p0, b0)
+        act(F("hie"), K(Bk[0]), bias=4096.0, scale=-1.0)
+        if rd == 0:
+            for lo, hi in PARTS:
+                tt(cols("mb", lo, hi), R("sow", M0, M0 + V), cols("sow", lo, hi, E), ALU.subtract, idx=sub(L("1"), lo, hi))
+                gcopy(cols("mb2", lo, hi), cols("mb", lo, hi))
+            for j in range(3):
+                mms(K(Bk[j], 0, CH), [(M("rev"), ch(p0, j)), (M("revc"), ch("cc", j))])
+                act(ch("tab", j, E), K(Bk[j], 0, CH))
+        else:
+            mstep("mb", "ma", R("ma2"), L("1"), copy="mb2")
+        hop("p2", R("p1"), L("2"), L("4"))
+        mstep("ma", "mb", R("mb2"), L("2"), copy="ma2")
+        merge("q4", M("q4"), "p1", "p2")
+        hop("p3", R("q4"), L("4"), L("8"))
+        mstep("mb", "ma", R("ma2"), L("4"), copy="mb2")
+        merge("q8", M("q8"), "q4", "p3")
+        hop("p4", R("q8"), L("8"), L("16"))
+        if rd == 0:
+            arrive(R("nsw"), "am0")
+            for j in range(3):
+                mms(K(W0, 0, CH), [(M("1"), ch("xn", j)), (M("-15/16"), ch("hi", j)), (M("1"), ch("nsw", j))])
+                act(ch("no0", j), K(W0, 0, CH))
+            act(F("nv"), nmask, scale=float(V))
+            tt(F("yb"), F("nv"), slot0, ALU.add)
+            tt(F("y2b"), slot1, F("nv"), ALU.subtract)
+            tt(F("same"), maskb, nmask, ALU.is_equal)
+            act(F("sm"), F("same"), bias=-FAR, scale=FAR)
+            act(F("sn"), F("same"), scale=-FAR)
+            act(B("hm"), nmask, bias=0.5, scale=-0.5)
+        wrap(Bk[0], Z("min"), "q8")
+        act(F("e0"), K(Bk[0]))
+        mstep("ma", "mb", R("mb2"), L("8"), copy="ma2")
+        wrap(Bk[1], Z("min"), "p4")
+        tt(F("e1"), K(Bk[1]), F("e0"), ALU.min)
+        hop("p5a", R("p4"), L("8"))
+        wrap(Bk[2], Z("min"), "p5a")
+        tt(F("e2"), K(Bk[2]), F("e1"), ALU.min)
+        mstep(m5, "ma", R("ma2"), L("16"))
+        dma("g", T.yw[:], T[m5][:], [R(m5)], [tag("yw")], add=rd == 1, lat=5000 + 2000 * rd)
+        for j in range(3):
+            mms(K(A[j], 0, CH), [(M("ev"), ch(p0, j, b0)), (M("ea"), ch("p5a", j))], stop=False)
+            mms(K(Bk[j], 0, CH), [(M("p4"), ch("p4", j)), (M("pa"), ch("p5a", j))], stop=False)
+        pv = CFG["p5"][rd]
+        for j, (lo, hi) in enumerate(THIRDS):
+            for l, h, eng in ((lo, min(hi, pv), cp), (max(lo, pv), hi, act)):
+                if l < h:
+                    eng(cols("p5b", l, h), R("p4"), idx=sub(L("16"), l, h))
+            mms(K(A[j], 0, CH), [(M("eb"), ch("p5b", j))], start=False)
+            mms(K(Bk[j], 0, CH), [(M("pb"), ch("p5b", j))], start=False)
+            if j in CFG["eqa"][rd]:
+                act(ch("h192", j), K(A[j], 0, CH), func=AF.Abs)
+                act(ch("eq", j), ch("h192", j), func=AF.Relu, bias=1.0, scale=-1.0)
+            else:
+                ts(ch("eq", j), K(A[j], 0, CH), 0.0, None, ALU.is_equal)
+            tt(ch("pp", j), K(Bk[j], 0, CH), ch("eq", j), ALU.mult)
+        cut = 72 - CFG["vsv"][rd]
+        for lo, hi in pairs(CFG["lg"]):
+            wrap(W1, Z("min"), "p5b", 0, lo, hi)
+            tt(sub(B("x", 4), lo, hi), K(W1, lo, hi), sub(F("e2"), lo, hi), ALU.min)
+            decode(W0, B("x"), lo, hi)
+            ts(sub(L("l"), lo, hi), K(W0, lo, hi), float(MID), None, ALU.add)
+            if lo < cut:
+                act(cols("vs", lo, min(hi, cut)), R(m5), func=AF.Sign, bias=-0.5, idx=sub(L("l"), lo, min(hi, cut)))
+            if hi > cut:
+                ts(cols("vs", max(lo, cut), hi), R(m5), 0.0, 2.0, ALU.is_gt, ALU.mult, idx=sub(L("l"), max(lo, cut), hi))
+        for k, (lo, hi) in enumerate(pairs(CFG["pg"])):
+            bc, bs = (A[0], Bk[0]) if k == 0 else (A[1], Bk[1])
+            mms(K(bc, lo, hi), [(M("1"), sub(B("eps"), lo, hi))] + wterms(Z("one"), "eq", 0, lo, hi))
+            recip(sub(F("rc"), lo, hi), K(bc, lo, hi))
+            act(sub(B("off"), lo, hi), K(bc, lo, hi), func=AF.Relu, bias=FAR, scale=-FAR)
+            wrap(bs, Z("one"), "pp", 0, lo, hi)
+            tt(sub(B("xp", 4), lo, hi), K(bs, lo, hi), sub(F("rc"), lo, hi), ALU.mult)
+            decode(bs, B("xp"), lo, hi)
+            if rd == 0:
+                ts(sub(F("pm"), lo, hi), K(bs, lo, hi), -1.0, 4096.0 - MID, ALU.mult, ALU.add)
+            act(sub(F("pe"), lo, hi), K(bs, lo, hi), bias=float(MID + E + V * rd))
+        mms(K(W1), [(M("-1"), B("off"))] + ([(M("1"), B("ind%d" % rd))] if cut < 72 else []), stop=False)
+        for lo, hi in pairs(CFG["lg"]):
+            wrap(W1, Z("vote"), "vs", 0, lo, hi, start=False, stop=hi == 72)
+
+    def pick(name, hi, lo, lst):
+        tt(F(name + "u"), K(W1), hi, ALU.min)
+        tt(F(name), F(name + "u"), lo, ALU.max)
+        if lst:
+            cp(lst, F(name))
+
+    def edges(lst, pieces, p0, b0):
+        pick("le", F("hie"), F("dumpk"), None)
+        ts(lst, F("le"), -1.0, 4096.0, ALU.mult, ALU.add)
+        for lo, hi in pairs(pieces):
+            tt(R("et"), cols(p0, lo, hi, b0), cols("cc", lo, hi), ALU.mult, oidx=sub(lst, lo, hi))
 
     walk(0)
-    ts(F("npf"), F("pf"), -1.0, -float(E), ALU.mult, ALU.add)
-    for k in range(2):
-        tt(half(F("q"), k), F("off"), half(F("mkn"), k), ALU.add)
-        tt(half(F("qm"), k), F("npf"), half(F("q"), k), ALU.add)
-    for k in range(2):
-        tt(half(F("u"), k), W("w1"), half(F("qm"), k), ALU.max)
-        tt(half(F("sl"), k), half(F("u"), k), half(F("slotm"), k), ALU.min)
-        ts(R("msgo", 72 * k, 72 * k + 72), half(F("sl"), k), -1.0, 0.25, ALU.mult, ALU.add)
+    tt(F("hy"), F("pe"), F("sm"), ALU.add)
+    tt(F("hy2"), F("pe"), F("sn"), ALU.add)
+    pick("sl", F("pm"), F("keepk"), None)
+    ts(R("msgo"), F("sl"), -1.0, 4096.0, ALU.mult, ALU.add)
     send(R("msgi"), R("msgo"), "amsg")
-    NV = CFG["nv"]
-    for j in list(range(NV, 6)) + list(range(NV)):
-        act(ch("so", j), R("sow"), idx=third(R("msgo"), j))
+    pick("y", F("hy"), F("yb"), L("y"))
+    pick("y2", F("hy2"), F("y2b"), L("y2"))
+    PC = pairs(CFG["pc"])
+    for lo, hi in PC:
+        act(cols("ys1", lo, hi), R("sow", 0, E + V), idx=sub(L("y"), lo, hi))
+    for lo, hi in PARTS:
+        tt(cols("pr2", lo, hi), R("sow", 0, E + V), cols("no0", lo, hi), ALU.mult, idx=sub(L("y2"), lo, hi))
+    for j, (lo, hi) in enumerate(PC[1:]):
+        mms(K(A[j], 0, 16 * (hi - lo)), [(M("1"), cols("ys1", lo, hi))])
+    mms(K(W0), [(M("1"), B("hm"))] + wterms(Z("neg"), "pr2", 0, 0, 72), stop=False)
+    tt(F("dy"), F("y"), F("y2"), ALU.subtract)
+    edges(L("e1"), CFG["sc"], "p0a", 0)
+    tt(F("t1"), nmask, F("dy"), ALU.mult)
+    tt(half(F("sk", 2), 0), F("y"), F("t1"), ALU.subtract)
+    tt(half(F("sk"), 1), F("y2"), F("t1"), ALU.add)
 
-    def sops(j):
-        return PS("psa" if j - NV < 3 else "psb", (j - NV) % 3)
-    for j in range(NV, 6):
-        mm(sops(j), MB(DI), ch("so", j), True, True)
-    turned()
-    tt(F("t1"), F("turn"), F("dce"), ALU.mult)
-    for k in range(2):
-        tt(half(fl, k), F("turn"), half(F("mk"), k), ALU.mult)
-    tt(F("t2"), F("t1"), F("dump"), ALU.add)
-    ts(half(F("u"), 0), half(fl, 0), float(E), None, ALU.mult)
-    ts(half(F("u"), 1), half(fl, 1), float(V), None, ALU.mult)
-    cp(LE1, F("t2"))
-    for k in range(2):
-        tt(half(F("u2"), k), F("pf"), half(F("hs"), k), ALU.subtract)
-    tt(F("tl"), F("u"), F("slot"), ALU.add)
-    tt(F("base"), F("u2"), fl, ALU.mult)
-    tt(F("dS"), half(F("sl"), 0), half(F("sl"), 1), ALU.subtract)
-    tt(F("dT"), half(F("tl"), 1), half(F("tl"), 0), ALU.subtract)
-    tt(F("hs2"), F("hs"), F("base"), ALU.add)
-    tt(F("dH"), half(F("hs2"), 1), half(F("hs2"), 0), ALU.subtract)
-    for lo, hi in zip(CFG["sc"][:-1], CFG["sc"][1:]):
-        scatter("p0a", LE1, lo, hi)
-
-    arrive(R("nsw", 0, E), "aso")
-    arrive(R("nsw", E, E + V), "am0")
     arrive(R("msgi"), "amsg")
-    for j in range(NV, 6):
-        act(ch("ng", j), R("nsw"), idx=third(R("msgi"), j))
-    for j in range(3):
-        act(ch("tab", j, E), R("p0a"), scale=GS, idx=third(LP, j))
-    for j in range(6):
-        if j < NV:
-            tt(ch("pr2", j), R("nsw"), ch("so", j), ALU.mult, idx=third(R("msgi"), j))
-        else:
-            tt(ch("pr2", j), sops(j), ch("ng", j), ALU.mult)
-    wrap(W("w0"), ZONE, "pr2", 0)
-    wrap(W("w1"), ZONE, "pr2", V)
-    cp(F("a0"), W("w0"))
-    tt(mask, W("w1"), F("a0"), ALU.is_gt)
-    tt(F("t0"), mask, F("dT"), ALU.mult)
-    tt(F("t2"), mask, F("dH"), ALU.mult)
-    tt(F("t3"), F("t0"), half(F("tl"), 0), ALU.add)
-    tt(F("t5"), F("t2"), half(F("hs2"), 0), ALU.add)
-    cp(LT, F("t3"))
-    tt(F("t1"), mask, F("dS"), ALU.mult)
-    tt(F("t4"), F("t1"), half(F("sl"), 0), ALU.subtract)
-    cvt(LC, F("t4"))
+    for j, (lo, hi) in enumerate(PC[1:]):
+        act(cols("ng", lo, hi), R("nsw"), idx=R("msgi", lo, hi))
+    lo, hi = PC[0]
+    tt(cols("pr", lo, hi), R("nsw"), cols("ys1", lo, hi), ALU.mult, idx=R("msgi", lo, hi))
+    for j, (lo, hi) in enumerate(PC[1:]):
+        tt(cols("pr", lo, hi), K(A[j], 0, 16 * (hi - lo)), cols("ng", lo, hi), ALU.mult)
+    wrap(W0, Z("one"), "pr", start=False)
+    ts(F("pk"), K(W0), 0.0, None, ALU.is_gt)
+    tt(F("t2"), F("pk"), F("dy"), ALU.mult)
+    tt(F("t3"), F("t2"), F("y2"), ALU.add)
+    cp(L("t"), F("t3"))
+    tt(F("mk2"), F("pk"), nmask, ALU.is_equal)
+    act(half(F("pen", 2), 0), F("mk2"), scale=-FAR)
+    act(half(F("pen"), 1), F("mk2"), bias=-FAR, scale=FAR)
     walk(1)
-    act(R("tab", E + V, 2 * E), R("p0b"), scale=GS, idx=LP)
-    tt(F("t8"), F("t7"), F("off"), ALU.add)
-    tt(F("t1"), W("w1"), F("t8"), ALU.max)
-    tt(F("t2"), F("t1"), F("dumpm"), ALU.min)
-    ts(LE2, F("t2"), 8192.0, None, ALU.add)
-    turned()
     for k in range(2):
-        tt(half(F("u"), k), F("turn"), half(F("q"), k), ALU.mult)
-    tt(F("base"), F("u"), F("tl"), ALU.add)
-    cp(R("ylu"), F("base"))
-    scatter("p0b", LE2, 0, 72)
+        tt(half(F("hk", 2), k), F("pe"), half(F("pen"), k), ALU.add)
+    edges(L("e2"), CFG["sc2"], "tab", E + V)
+    for k in range(2):
+        pick("f%d" % k, half(F("hk"), k), half(F("sk"), k), R("ylu", 72 * k, 72 * k + 72))
 
-    def rows_out(out, w, z, data, stage):
-        for j in range(16):
-            mm(W(w, 0, 144), zsel(z, j), R(data, 144 * j, 144 * j + 144), j == 0, j == 15)
-        act(stage, W(w, 0, 144))
-        dma("a", out[:], ap(stage), [stage], [tag(w + "out")], lat=2400)
+    def rows_out(out, b, z, data, stage, extra=()):
+        mms(K(b, 0, 144), [((z[0], z[1] + 15 - j, z[1] + 143 - j, 1), R(data, 144 * j, 144 * j + 144)) for j in range(16)])
+        act(stage, K(b, 0, 144))
+        dma("a", out[:], ap(stage), [stage], [tag("out", b)], lat=2400)
     for k in range(2):
         act(R("yg", V * k, V * k + V), R("tab"), idx=R("ylu", 72 * k, 72 * k + 72))
-    rows_out(T.yl, "w0", ZEDGE, "yg", F("sl"))
+    rows_out(T.yl, W0, Z("edge"), "yg", F("sk"))
     lo = 0
     for j in range(6):
-        ps = PS("psa" if j < 3 else "psb", j % 3)
-        mm(ps, MB(MSG), ch("ew", j), True, True)
-        tt(ch("yso", j), ps, ch("spb", j), ALU.mult)
+        mms(K(j, 0, CH), [(M("sg"), ch("et", j))])
+        tt(ch("yso", j), K(j, 0, CH), ch("spb", j), ALU.mult)
         if j in CFG["ysc"]:
             dma("s", T.ys[:, CH * lo:CH * (j + 1)], T.yso[:, CH * lo:CH * (j + 1)],
                 [R("yso", CH * lo, CH * (j + 1))], [tag("ys", j)], lat=2200 + 400 * (j + 1 - lo))
             lo = j + 1
-    rows_out(T.yh, "w1", ZH89, "ew", F("slotm"))
+    rows_out(T.yh, W1, Z("h"), "et", F("pen"))
 
     emit(g, T, schedule(ops), n_in, n_out)
 
@@ -599,6 +622,9 @@ def schedule(ops):
                 ps.append(last["x"])
             o["lat"] = ops[last[o["sem"]]]["lat"] - 2000
             last["x"] = i
+        for j in o.get("after", ()):
+            pred[i].append((j, ops[j]["t"]))
+            succ[j].append((i, ops[j]["t"]))
         for j in ps:
             pred[i].append((j, gap(j, i)))
             succ[j].append((i, gap(j, i)))

@@ -8,20 +8,30 @@ FAR = 1048576.0
 MID = 576
 KNOTS = ((0, 8), (64, 4), (192, 2), (320, 1), (448, 1), (576, 1), (704, 1), (832, 2), (960, 4), (1088, 8), (1152, 0))
 BF, F32, F16, I32, U16 = "bfloat16", "float32", "float16", "int32", "uint16"
-EST = dict(cyc=0.9, gath=1.55, scat=3.8, pe=0.45, wake=100, link=70.0, rounds=1000, sig=1500.0, win=4000.0, seed=1)
+EST = dict(cyc=0.85, gath=1.55, scat=3.8, pe=0.45, wake=150, link=80.0, rounds=60, sig=1500.0, win=4000.0,
+           heat=250.0, moves=30000, seed=1,
+           cases=(dict(wake=0, r=1, x=1, d=1), dict(g=1.5, s=1.0, c=1.2, p=1.15, wake=60, r=1.2, x=1.25, d=1.1),
+                  dict(g=0.95, s=1.6, c=1.2, p=1.15, wake=100, r=0.9, x=0.8, d=0.9)))
 CFG = dict(
     ha=36,
-    sc=(0, 12, 24, 36, 48, 60, 72),
-    sc2=(0, 24, 72),
-    xc=(0, 8, 32, 56, 72),
+    sc=(0, 10, 20, 30, 40, 50, 60, 72),
+    sc2=(0, 12, 72),
+    xc=(0, 12, 42, 72),
     lg=(0, 72),
     pg=(0, 72),
     pc=(0, 30, 52, 72),
     m0=(72, 72),
     p5=(0, 0),
-    eqa=((), ()),
+    eqa=((0, 1), (0, 1)),
     vsv=(0, 0),
-    ysc=(1, 3, 5),
+    whole=("p2", "p3", "p4"),
+    tw=((("v", 0),) * 3 + (("v", 10),) * 2,) * 2,
+    s0=128,
+    s1=1152,
+    p2a=1,
+    thirds=(),
+    nega=(),
+    ysc=(0, 2, 4, 5),
 )
 
 
@@ -35,12 +45,12 @@ SB = {
     "hdi": (144, I32), "hdd": (288, I32), "hdb": (432, BF), "hu": (576, F16),
     "et": (E + V, BF), "ct": (V, BF), "cc": (V, BF), "tab": (2 * E, BF),
     "a16": (V, BF), "xo": (V, BF), "xn": (V, BF), "h192": (V, BF), "hi": (V, BF),
-    "pa16": (V, F16), "pb16": (V, F16), "sow": (2 * E + 80, BF), "nsw": (E + 80, BF),
+    "pa16": (V, F16), "pb16": (V, F16), "sow": (2 * E + 80, BF), "nsw": (E + V + 80, BF),
     "no0": (V, BF), "ys1": (V, BF), "ng": (V, BF), "pr": (V, BF), "pr2": (V, BF),
     "p0a": (V, BF), "p1": (V, BF), "p2": (V, BF), "q4": (V, BF), "p3": (V, BF), "q8": (V, BF), "p4": (V, BF),
     "p5a": (V, BF), "p5b": (V, BF),
     "ma": (V, BF), "mb": (V, BF), "ma2": (V, BF), "mb2": (V, BF), "m5a": (V, BF), "m5b": (V, BF),
-    "eq": (V, BF), "pp": (V, BF), "vs": (V, BF), "yg": (E, BF), "yso": (E, BF),
+    "eq": (V, BF), "pp": (V, BF), "vs": (V, BF), "yg": (E, BF), "yso": (E, BF), "wsum": (V, F32),
     "lst": (72 * 14, U16), "msgo": (72, U16), "msgi": (72, U16), "ylu": (144, U16),
     "wf": (72 * 64, F32), "wb": (72 * 16, BF),
     "pi": (4, I32), "col": (64, F32), "oh": (16, F32), "jf": (144, F32), "jb": (144, BF), "b128": (18, F32),
@@ -51,7 +61,7 @@ SCRATCH = {k: ("sbuf", [128, n], d) for k, (n, d) in SB.items()}
 PSUM = ["k%d" % i for i in range(8)]
 SCRATCH.update({k: ("psum", [128, 512], F32) for k in PSUM})
 NDMA = 24
-SEMAPHORES = (["cv", "ca", "cp", "cg", "lsent", "ax0", "ax1", "ax2", "ax3", "am0", "amsg"]
+SEMAPHORES = (["cv", "ca", "cp", "cg", "lsent", "ax0", "ax1", "ax2", "ax3", "am0", "as0", "as1", "as2", "amsg"]
               + ["d%d" % i for i in range(NDMA)])
 
 
@@ -99,7 +109,9 @@ def rank_program(g, core, T, topo):
     def op(q, fn, reads, writes, kind="c", **kw):
         rd = [span(r) for r in reads if r[0] not in PSUM]
         wr = [span(r) for r in writes] + [span(r) for r in reads if r[0] in PSUM]
-        ops.append(dict(q=q, fn=fn, rd=rd, wr=wr, kind=kind, **kw))
+        listed = any(r[0] in ("lst", "lvu", "msgi", "ylu") for r in reads) and writes[0][0] != "lvu"
+        sort = "s" if listed and writes[0][0] == "et" else "g" if listed else "p" if q == "p" else kind
+        ops.append(dict(q=q, fn=fn, rd=rd, wr=wr, kind=kind, sort=sort if kind == "c" else "", **kw))
 
     def sc(x):
         return ap(x) if isinstance(x, tuple) else x
@@ -160,7 +172,8 @@ def rank_program(g, core, T, topo):
 
     def send(dst, srcr, sem, nbytes=2):
         op("g", lambda: g.remote_dma(ap(dst), ap(srcr), T.sem[sem], T.sem.lsent, pid, rid, out_mask), [srcr], [], kind="r",
-           t=400, sem=sem, lat=2700 + width(srcr) * 128 * nbytes / EST["link"])
+           t=400 + 1500 * (sem == "as0"), sem=sem,
+           lat=2880 + {"as0": 1500, "am0": 1000, "amsg": -300}.get(sem, 0) + width(srcr) * 128 * nbytes / EST["link"])
 
     def arrive(dst, sem):
         op("x", None, [], [dst], kind="x", sem=sem, t=0)
@@ -230,10 +243,14 @@ def rank_program(g, core, T, topo):
     maskb, nmask = R("sow", E + V, E + V + 72), R("nsw", V, V + 72)
 
     sp0 = R("spb")
-    dma("s", T.lvi[:], T.lv[:], [], [R("lvi")], lat=2300)
-    dma("a", T.hdi[:], T.hd[:], [], [R("hdi")], lat=2300)
-    dma("s", T.spb[:], T.sp[:], [], [sp0], lat=4400)
-    ops[2]["after"] = [0, 1]
+    dma("s", T.lvi[:], T.lv[:], [], [R("lvi")], lat=2600)
+    dma("a", T.hdi[:], T.hd[:], [], [R("hdi")], lat=2600)
+    S0 = CFG["s0"]
+    dma("s", T.spb[:, 0:S0], T.sp[:, 0:S0], [], [R("spb", 0, S0)], lat=2600)
+    dma("s", T.spb[:, S0:E], T.sp[:, S0:E], [], [R("spb", S0)], lat=5600)
+    ops[3]["after"] = [0, 1, 2]
+    send(R("nsw", V + 80, V + 80 + S0), R("spb", 0, S0), "as0")
+    arrive(R("nsw", V + 80, V + 80 + S0), "as0")
 
     iota(R("pi", 0, 1), [[0, 1]], 0, 1)
     iota(R("jf"), [[1, 144]], 0, 0)
@@ -292,7 +309,6 @@ def rank_program(g, core, T, topo):
     act(slot0, R("i16"), bias=RF)
     act(slot1, slot0, bias=float(V))
     act(F("dumpk"), slot0, bias=4096.0 - E, scale=-1.0)
-    act(F("keepk"), slot0, bias=4096.0 - V - 80, scale=-1.0)
     ts(DD, JB, C15, 15.0, ALU.subtract, ALU.add)
     ts(DN, DD, 0.0, 200.0, ALU.is_lt, ALU.mult)
     tt(DM, DD, DN, ALU.add)
@@ -367,6 +383,9 @@ def rank_program(g, core, T, topo):
 
     for j, (lo, hi) in enumerate(XC):
         arrive(cols("xn", lo, hi), "ax%d" % j)
+    S1 = CFG["s1"]
+    send(R("nsw", V + 80 + S0, V + 80 + S1), R("spb", S0, S1), "as1")
+    ops[-1]["rd"].append(span(R("xn")))
     for j, (lo, hi) in enumerate(XC):
         tt(cols("pa16", lo, hi), xk(A, j), cols("xn", lo, hi), ALU.mult)
         ts(cols("hi", lo, hi), cols("xn", lo, hi), 1.5 * 2 ** 27, 1.5 * 2 ** 27, ALU.add, ALU.subtract)
@@ -379,18 +398,29 @@ def rank_program(g, core, T, topo):
     act(maskb, F("t0"), scale=1.0 / V)
     fill(R("sow", E + V + 72, M0), 0.0)
 
-    def mstep(out, win, dup, idx, o=ALU.add, copy=None):
-        for lo, hi in PARTS:
-            tt(cols(out, lo, hi), R(win), sub(dup, 16 * lo, 16 * hi), o, idx=sub(idx, lo, hi))
+    def twin(copy, out, lo, hi, how):
+        who, k = how
+        gcopy(cols(copy, lo, hi - k), cols(out, lo, hi - k))
+        if k:
+            (cp if who == "v" else act)(cols(copy, hi - k, hi), cols(out, hi - k, hi))
+
+    def mstep(out, win, dup, idx, copy=None, how=None):
+        for k, (lo, hi) in enumerate(PARTS):
+            tt(cols(out, lo, hi), R(win), sub(dup, 16 * lo, 16 * hi), ALU.add, idx=sub(idx, lo, hi))
             if copy:
-                gcopy(cols(copy, lo, hi), cols(out, lo, hi))
+                twin(copy, out, lo, hi, how)
 
     def hop(out, win, idx, lst=None, base=0, parts=PARTS):
+        whole = out in CFG["whole"]
+        parts = THIRDS if out in CFG["thirds"] else parts
         for k, (lo, hi) in enumerate(parts):
             act(cols(out, lo, hi, base), win, idx=sub(idx, lo, hi))
-            if lst:
+            if lst and not whole:
                 wrap((W0, W1)[k], Z("head"), out, base, lo, hi)
                 cp(sub(lst, lo, hi), K((W0, W1)[k], lo, hi))
+        if lst and whole:
+            wrap(W1, Z("head"), out, base)
+            cp(lst, K(W1))
 
     def merge(out, m, before, shifted):
         for j in range(3):
@@ -405,43 +435,46 @@ def rank_program(g, core, T, topo):
     def walk(rd):
         p0, b0, m5 = ("p0a", 0, "m5a") if rd == 0 else ("tab", E + V, "m5b")
         m0, c0 = ("sow", M0) if rd == 0 else ("ma", 0)
-        win = E + V * rd
+        win, tw = E + V * rd, CFG["tw"][rd]
         hop(p0, R("tab", 0, win), L("t"), L("1"), b0)
         mv = CFG["m0"][rd]
         for lo, hi in PARTS:
             for l, h, eng in ((lo, min(hi, mv), cp), (max(lo, mv), hi, act)):
                 if l < h:
                     eng(cols(m0, l, h, c0), R("sow", 0, win), idx=sub(L("t"), l, h))
-            if rd == 0:
+            if rd == 0 and lo in CFG["nega"]:
+                act(cols("sow", lo, hi, E), cols(m0, lo, hi, c0), scale=-1.0)
+            elif rd == 0:
                 ts(cols("sow", lo, hi, E), cols(m0, lo, hi, c0), -1.0, None, ALU.mult)
             else:
-                gcopy(cols("ma2", lo, hi), cols("ma", lo, hi))
+                twin("ma2", "ma", lo, hi, tw[0])
         if rd == 0:
-            send(R("nsw"), R("sow", E, 2 * E + 80), "am0")
+            send(R("nsw", 0, V + 80), R("sow", E, M0), "am0")
+            send(R("nsw", V + 80 + S1), R("spb", S1), "as2")
         hop("p1", R(p0, b0, b0 + V), L("1"), L("2"))
         wrap(Bk[0], Z("edge"), p0, b0)
         act(F("hie"), K(Bk[0]), bias=4096.0, scale=-1.0)
         if rd == 0:
+            act(F("keepk"), K(Bk[0]), bias=4096.0 - V - 80, scale=-1.0)
             for lo, hi in PARTS:
                 tt(cols("mb", lo, hi), R("sow", M0, M0 + V), cols("sow", lo, hi, E), ALU.subtract, idx=sub(L("1"), lo, hi))
-                gcopy(cols("mb2", lo, hi), cols("mb", lo, hi))
+                twin("mb2", "mb", lo, hi, tw[1])
             for j in range(3):
                 mms(K(Bk[j], 0, CH), [(M("rev"), ch(p0, j)), (M("revc"), ch("cc", j))])
                 act(ch("tab", j, E), K(Bk[j], 0, CH))
         else:
-            mstep("mb", "ma", R("ma2"), L("1"), copy="mb2")
+            mstep("mb", "ma", R("ma2"), L("1"), "mb2", tw[1])
         hop("p2", R("p1"), L("2"), L("4"))
-        mstep("ma", "mb", R("mb2"), L("2"), copy="ma2")
+        mstep("ma", "mb", R("mb2"), L("2"), "ma2", tw[2])
         merge("q4", M("q4"), "p1", "p2")
         hop("p3", R("q4"), L("4"), L("8"))
-        mstep("mb", "ma", R("ma2"), L("4"), copy="mb2")
+        mstep("mb", "ma", R("ma2"), L("4"), "mb2", tw[3])
         merge("q8", M("q8"), "q4", "p3")
         hop("p4", R("q8"), L("8"), L("16"))
         if rd == 0:
-            arrive(R("nsw"), "am0")
-            for j in range(3):
-                mms(K(W0, 0, CH), [(M("1"), ch("xn", j)), (M("-15/16"), ch("hi", j)), (M("1"), ch("nsw", j))])
-                act(ch("no0", j), K(W0, 0, CH))
+            arrive(R("nsw", V + 80 + S0, V + 80 + S1), "as1")
+            arrive(R("nsw", 0, V + 80), "am0")
+            arrive(R("nsw", V + 80 + S1), "as2")
             act(F("nv"), nmask, scale=float(V))
             tt(F("yb"), F("nv"), slot0, ALU.add)
             tt(F("y2b"), slot1, F("nv"), ALU.subtract)
@@ -449,19 +482,20 @@ def rank_program(g, core, T, topo):
             act(F("sm"), F("same"), bias=-FAR, scale=FAR)
             act(F("sn"), F("same"), scale=-FAR)
             act(B("hm"), nmask, bias=0.5, scale=-0.5)
-        wrap(Bk[0], Z("min"), "q8")
-        act(F("e0"), K(Bk[0]))
-        mstep("ma", "mb", R("mb2"), L("8"), copy="ma2")
-        wrap(Bk[1], Z("min"), "p4")
-        tt(F("e1"), K(Bk[1]), F("e0"), ALU.min)
+        wrap(W0, Z("min"), "q8")
+        act(F("e0"), K(W0))
+        mstep("ma", "mb", R("mb2"), L("8"), "ma2", tw[4])
+        wrap(W0, Z("min"), "p4")
+        tt(F("e1"), K(W0), F("e0"), ALU.min)
         hop("p5a", R("p4"), L("8"))
-        wrap(Bk[2], Z("min"), "p5a")
-        tt(F("e2"), K(Bk[2]), F("e1"), ALU.min)
+        wrap(W0, Z("min"), "p5a")
+        tt(F("e2"), K(W0), F("e1"), ALU.min)
         mstep(m5, "ma", R("ma2"), L("16"))
-        dma("g", T.yw[:], T[m5][:], [R(m5)], [tag("yw")], add=rd == 1, lat=5000 + 2000 * rd)
         for j in range(3):
-            mms(K(A[j], 0, CH), [(M("ev"), ch(p0, j, b0)), (M("ea"), ch("p5a", j))], stop=False)
-            mms(K(Bk[j], 0, CH), [(M("p4"), ch("p4", j)), (M("pa"), ch("p5a", j))], stop=False)
+            mms(K(A[j], 0, CH), [(M("ev"), ch(p0, j, b0))], stop=False)
+            mms(K(Bk[j], 0, CH), [(M("p4"), ch("p4", j))], stop=False)
+            mms(K(A[j], 0, CH), [(M("ea"), ch("p5a", j))], start=False, stop=False)
+            mms(K(Bk[j], 0, CH), [(M("pa"), ch("p5a", j))], start=False, stop=False)
         pv = CFG["p5"][rd]
         for j, (lo, hi) in enumerate(THIRDS):
             for l, h, eng in ((lo, min(hi, pv), cp), (max(lo, pv), hi, act)):
@@ -494,8 +528,17 @@ def rank_program(g, core, T, topo):
             tt(sub(B("xp", 4), lo, hi), K(bs, lo, hi), sub(F("rc"), lo, hi), ALU.mult)
             decode(bs, B("xp"), lo, hi)
             if rd == 0:
-                ts(sub(F("pm"), lo, hi), K(bs, lo, hi), -1.0, 4096.0 - MID, ALU.mult, ALU.add)
+                act(sub(F("pm"), lo, hi), K(bs, lo, hi), bias=4096.0 - MID, scale=-1.0)
             act(sub(F("pe"), lo, hi), K(bs, lo, hi), bias=float(MID + E + V * rd))
+        if rd == 0:
+            for j, b in enumerate((A[1], A[2], Bk[2])):
+                mms(K(b, 0, CH), [(M("1"), ch("xn", j)), (M("-15/16"), ch("hi", j)), (M("1"), ch("nsw", j))])
+                act(ch("no0", j), K(b, 0, CH))
+        else:
+            for j, b in enumerate((A[1], A[2], Bk[2])):
+                mms(K(b, 0, CH), [(M("1"), ch("m5a", j)), (M("1"), ch("m5b", j))])
+                act(ch("wsum", j), K(b, 0, CH))
+            dma("s", T.yw[:], T.wsum[:], [R("wsum")], [tag("yw")], lat=8000)
         mms(K(W1), [(M("-1"), B("off"))] + ([(M("1"), B("ind%d" % rd))] if cut < 72 else []), stop=False)
         for lo, hi in pairs(CFG["lg"]):
             wrap(W1, Z("vote"), "vs", 0, lo, hi, start=False, stop=hi == 72)
@@ -523,8 +566,13 @@ def rank_program(g, core, T, topo):
     PC = pairs(CFG["pc"])
     for lo, hi in PC:
         act(cols("ys1", lo, hi), R("sow", 0, E + V), idx=sub(L("y"), lo, hi))
-    for lo, hi in PARTS:
-        tt(cols("pr2", lo, hi), R("sow", 0, E + V), cols("no0", lo, hi), ALU.mult, idx=sub(L("y2"), lo, hi))
+    for j, (lo, hi) in enumerate(THIRDS):
+        if j < CFG["p2a"]:
+            act(cols("h192", lo, hi), R("sow", 0, E + V), idx=sub(L("y2"), lo, hi))
+            mms(K(Bk[j], 0, CH), [(M("1"), ch("no0", j))])
+            tt(ch("pr2", j), K(Bk[j], 0, CH), ch("h192", j), ALU.mult)
+        else:
+            tt(cols("pr2", lo, hi), R("sow", 0, E + V), cols("no0", lo, hi), ALU.mult, idx=sub(L("y2"), lo, hi))
     for j, (lo, hi) in enumerate(PC[1:]):
         mms(K(A[j], 0, 16 * (hi - lo)), [(M("1"), cols("ys1", lo, hi))])
     mms(K(W0), [(M("1"), B("hm"))] + wterms(Z("neg"), "pr2", 0, 0, 72), stop=False)
@@ -557,9 +605,11 @@ def rank_program(g, core, T, topo):
         pick("f%d" % k, half(F("hk"), k), half(F("sk"), k), R("ylu", 72 * k, 72 * k + 72))
 
     def rows_out(out, b, z, data, stage, extra=()):
-        mms(K(b, 0, 144), [((z[0], z[1] + 15 - j, z[1] + 143 - j, 1), R(data, 144 * j, 144 * j + 144)) for j in range(16)])
+        for lo in (0, 8):
+            mms(K(b, 0, 144), [((z[0], z[1] + 15 - j, z[1] + 143 - j, 1), R(data, 144 * j, 144 * j + 144)) for j in range(lo, lo + 8)],
+                lo == 0, lo == 8)
         act(stage, K(b, 0, 144))
-        dma("a", out[:], ap(stage), [stage], [tag("out", b)], lat=2400)
+        dma("a", out[:], ap(stage), [stage], [tag("out", b)], lat=4200 if b == W0 else 3000)
     for k in range(2):
         act(R("yg", V * k, V * k + V), R("tab"), idx=R("ylu", 72 * k, 72 * k + 72))
     rows_out(T.yl, W0, Z("edge"), "yg", F("sk"))
@@ -569,7 +619,7 @@ def rank_program(g, core, T, topo):
         tt(ch("yso", j), K(j, 0, CH), ch("spb", j), ALU.mult)
         if j in CFG["ysc"]:
             dma("s", T.ys[:, CH * lo:CH * (j + 1)], T.yso[:, CH * lo:CH * (j + 1)],
-                [R("yso", CH * lo, CH * (j + 1))], [tag("ys", j)], lat=2200 + 400 * (j + 1 - lo))
+                [R("yso", CH * lo, CH * (j + 1))], [tag("ys", j)], lat=2200 + 400 * (6 - lo))
             lo = j + 1
     rows_out(T.yh, W1, Z("h"), "et", F("pen"))
 
@@ -620,7 +670,7 @@ def schedule(ops):
             ps.append(last[o["sem"]])
             if "x" in last:
                 ps.append(last["x"])
-            o["lat"] = ops[last[o["sem"]]]["lat"] - 2000
+            o["lat"] = ops[last[o["sem"]]]["lat"] - 2400
             last["x"] = i
         for j in o.get("after", ()):
             pred[i].append((j, ops[j]["t"]))
@@ -634,48 +684,131 @@ def schedule(ops):
         start = [0.0] * n
         busy = {q: [] for q in "vapgsx"}
         for i in order:
-            d = ops[i]["t"]
+            d = dur[i]
             if forward:
-                t = max([start[j] + w for j, w in pred[i]], default=0.0)
+                t = 0.0
+                for j, w in pred[i]:
+                    if start[j] + w > t:
+                        t = start[j] + w
             else:
-                t = max([start[j] + ops[j]["t"] + w - d for j, w in succ[i]] + [tail[i] - d])
-            b = busy[ops[i]["q"]]
-            at = len(b)
-            for k in range(len(b)):
-                s, e = b[k]
-                if e <= t:
-                    continue
-                if t + d <= s:
-                    at = k
-                    break
-                t = e
-            b.insert(at, (t, t + d))
+                t = tail[i] - d
+                for j, w in succ[i]:
+                    if start[j] + dur[j] + w - d > t:
+                        t = start[j] + dur[j] + w - d
+            b = busy[que[i]]
+            k = len(b)
+            while k and b[k - 1][1] > t:
+                k -= 1
+            while k < len(b) and t + d > b[k][0]:
+                t = max(t, b[k][1])
+                k += 1
+            b.insert(k, (t, t + d))
             start[i] = t
         return start
 
     state = [EST["seed"]]
+    dur = [o["t"] for o in ops]
+    que = [o["q"] for o in ops]
+    for lst in pred + succ:
+        lst[:] = list({j: max(w for k, w in lst if k == j) for j, _ in lst}.items())
 
     def draw():
         state[0] = (state[0] * 6364136223846793005 + 1442695040888963407) % (1 << 64)
         return (state[0] >> 33) / float(1 << 31)
-    best, order = None, list(range(n))
-    for _ in range(EST["rounds"]):
+    best, cur, order = None, None, list(range(n))
+    for r in range(EST["rounds"]):
         for _ in range(2):
             st = place(order, True)
             end = max(st[i] + tail[i] for i in range(n))
             if best is None or end <= best[0]:
                 best = (end, sorted(range(n), key=lambda i: (st[i], i)), st)
-            back = place(sorted(range(n), key=lambda i: (-(st[i] + ops[i]["t"]), -i)), False)
-            order = sorted(range(n), key=lambda i: (-(back[i] + ops[i]["t"]), i))
-        t0 = draw() * best[0]
-        key = [s + ((draw() + draw() + draw() - 1.5) * 2 * EST["sig"] if abs(s - t0) < EST["win"] else 0.0) for s in best[2]]
+            if cur is None or end <= cur[0] + EST["heat"] * (1 - r / EST["rounds"]) * draw():
+                cur = (end, st)
+            back = place(sorted(range(n), key=lambda i: (-(st[i] + dur[i]), -i)), False)
+            order = sorted(range(n), key=lambda i: (-(back[i] + dur[i]), i))
+        t0, sig = draw() * cur[0], EST["sig"] * (0.3 + draw())
+        key = [s + ((draw() + draw() + draw() - 1.5) * 2 * sig if abs(s - t0) < EST["win"] else 0.0) for s in cur[1]]
         for i in range(n):
             for j, w in pred[i]:
                 if key[i] <= key[j]:
                     key[i] = key[j] + 1e-3
         order = sorted(range(n), key=lambda i: key[i])
+
+    anc = [0] * n
+    for i in range(n):
+        for j, w in pred[i]:
+            anc[i] |= anc[j] | 1 << j
+    lean = [[(j, w) for j, w in pred[i]
+             if ops[j]["kind"] != "c" or not any(anc[k] >> j & 1 and v >= EST["wake"] for k, v in pred[i])] for i in range(n)]
+
+    cases = []
+    for f in EST["cases"]:
+        d = [o["t"] * f.get(o["sort"], 1.0) for o in ops]
+        cases.append((d, [[(j, w - dur[j] + d[j] + f["wake"] * (w > dur[j]) if ops[j]["kind"] == "c" else w * f[ops[j]["kind"]])
+                           for j, w in lean[i]] for i in range(n)]))
+
+    def run1(seq, dur, lean):
+        start, by_whom, free, on = [0.0] * n, [-1] * n, dict.fromkeys("vapgsx", 0.0), dict.fromkeys("vapgsx", -1)
+        end, last_i = 0.0, 0
+        for i in seq:
+            q = que[i]
+            t, who = free[q], on[q]
+            for j, w in lean[i]:
+                if start[j] + w > t:
+                    t, who = start[j] + w, j
+            start[i], by_whom[i], free[q], on[q] = t, who, t + dur[i], i
+            if t + tail[i] > end:
+                end, last_i = t + tail[i], i
+        return end + sum(start) / n, start, by_whom, last_i, end
+
+    def run(seq):
+        res = [run1(seq, d, e) for d, e in cases]
+        return sum(x[0] for x in res) / len(res), res[0][1], res, None, res[0][4]
+    seq = best[1]
+    now = run(seq)
+    best = (now[0], seq)
+    for r in range(EST["moves"]):
+        case = now[2][int(draw() * len(cases))]
+        chain, i = [], case[3] if draw() < 0.5 else int(draw() * n)
+        while case[2][i] >= 0:
+            j = case[2][i]
+            if que[j] == que[i] and not anc[i] >> j & 1:
+                chain.append((j, i))
+            i = j
+        if not chain:
+            continue
+        u, v = chain[int(draw() * len(chain))]
+        a, b = seq.index(u), seq.index(v)
+        hops = int(draw() ** 2 * 4)
+        if draw() < 0.5:
+            while hops and a > 0:
+                a -= 1
+                if que[seq[a]] == que[v]:
+                    if anc[v] >> seq[a] & 1:
+                        a += 1
+                        break
+                    hops -= 1
+            mid = seq[a:b + 1]
+            new = [x for x in mid if x == v or anc[v] >> x & 1] + [x for x in mid if x != v and not anc[v] >> x & 1]
+        else:
+            while hops and b < n - 1:
+                b += 1
+                if que[seq[b]] == que[u]:
+                    if anc[seq[b]] >> u & 1:
+                        b -= 1
+                        break
+                    hops -= 1
+            mid = seq[a:b + 1]
+            new = [x for x in mid if x != u and not anc[x] >> u & 1] + [x for x in mid if x == u or anc[x] >> u & 1]
+        cand = seq[:a] + new + seq[b + 1:]
+        res = run(cand)
+        if res[0] <= now[0] + EST["heat"] * (1 - r / EST["moves"]) * draw() ** 2:
+            place_of = {x: k for k, x in enumerate(cand)}
+            seq, now = sorted(cand, key=lambda x: (res[1][x], place_of[x])), res
+            if res[0] < best[0]:
+                best = (res[0], seq)
     ORDER[n] = best[1]
-    ORDER["end"] = best[0]
+    ORDER["end"] = run(best[1])[4]
     return [ops[i] for i in best[1]]
 
 

from concourse.mybir import AluOpType as ALU, ActivationFunctionType as AF

V = 1152
E = 2304
CH = 384
BIG = 16384.0
FAR = 1048576.0
MID = 576
KNOTS = ((0, 8), (64, 4), (192, 2), (320, 1), (448, 1), (576, 1), (704, 1), (832, 2), (960, 4), (1088, 8), (1152, 0))
BF, F32, F16, I32, U16 = "bfloat16", "float32", "float16", "int32", "uint16"
EST = dict(cyc=0.85, gath=1.55, scat=3.8, pe=0.45, wake=150, link=80.0, rounds=60, sig=1500.0, win=4000.0,
           heat=250.0, moves=30000, seed=1,
           cases=(dict(wake=0, r=1, x=1, d=1), dict(g=1.5, s=1.0, c=1.2, p=1.15, wake=60, r=1.2, x=1.25, d=1.1),
                  dict(g=0.95, s=1.6, c=1.2, p=1.15, wake=100, r=0.9, x=0.8, d=0.9)))
CFG = dict(
    ha=36,
    sc=(0, 10, 20, 30, 40, 50, 60, 72),
    sc2=(0, 12, 72),
    xc=(0, 12, 42, 72),
    lg=(0, 72),
    pg=(0, 72),
    pc=(0, 30, 52, 72),
    m0=(72, 72),
    p5=(0, 0),
    eqa=((0, 1), (0, 1)),
    vsv=(0, 0),
    whole=("p2", "p3", "p4"),
    tw=((("v", 0),) * 3 + (("v", 10),) * 2,) * 2,
    s0=128,
    s1=1152,
    p2a=1,
    thirds=(),
    nega=(),
    ysc=(0, 2, 4, 5),
)


def coded(v):
    u = v - MID
    return 8 * u - 4 * max(-512, min(512, u)) - 2 * max(-384, min(384, u)) - max(-256, min(256, u))


SB = {
    "spb": (E, BF), "lvi": (144, I32), "lvu": (144, U16),
    "hdi": (144, I32), "hdd": (288, I32), "hdb": (432, BF), "hu": (576, F16),
    "et": (E + V, BF), "ct": (V, BF), "cc": (V, BF), "tab": (2 * E, BF),
    "a16": (V, BF), "xo": (V, BF), "xn": (V, BF), "h192": (V, BF), "hi": (V, BF),
    "pa16": (V, F16), "pb16": (V, F16), "sow": (2 * E + 80, BF), "nsw": (E + V + 80, BF),
    "no0": (V, BF), "ys1": (V, BF), "ng": (V, BF), "pr": (V, BF), "pr2": (V, BF),
    "p0a": (V, BF), "p1": (V, BF), "p2": (V, BF), "q4": (V, BF), "p3": (V, BF), "q8": (V, BF), "p4": (V, BF),
    "p5a": (V, BF), "p5b": (V, BF),
    "ma": (V, BF), "mb": (V, BF), "ma2": (V, BF), "mb2": (V, BF), "m5a": (V, BF), "m5b": (V, BF),
    "eq": (V, BF), "pp": (V, BF), "vs": (V, BF), "yg": (E, BF), "yso": (E, BF), "wsum": (V, F32),
    "lst": (72 * 14, U16), "msgo": (72, U16), "msgi": (72, U16), "ylu": (144, U16),
    "wf": (72 * 64, F32), "wb": (72 * 16, BF),
    "pi": (4, I32), "col": (64, F32), "oh": (16, F32), "jf": (144, F32), "jb": (144, BF), "b128": (18, F32),
    "cb1": (18, F32), "cb3": (18, F32), "dd": (128 * 3, BF),
    "zb": (144 * 7, BF), "zh": (144, F16), "mb16": (128 * 24, BF), "mh16": (128 * 4, F16), "i16": (72, F32),
}
SCRATCH = {k: ("sbuf", [128, n], d) for k, (n, d) in SB.items()}
PSUM = ["k%d" % i for i in range(8)]
SCRATCH.update({k: ("psum", [128, 512], F32) for k in PSUM})
NDMA = 24
SEMAPHORES = (["cv", "ca", "cp", "cg", "lsent", "ax0", "ax1", "ax2", "ax3", "am0", "as0", "as1", "as2", "amsg"]
              + ["d%d" % i for i in range(NDMA)])


def rank_program(g, core, T, topo):
    rank = T.rank_of(core)
    if rank is None:
        return
    n = len(T.cores)
    prev, nxt = T.cores[(rank - 1) % n], T.cores[(rank + 1) % n]
    rid, pid = topo.addr(prev, core)
    out_mask, n_out, n_in = topo.mask(core, prev), len(topo.engines(core, prev)), len(topo.engines(nxt, core))

    ops = []
    CYC = EST["cyc"]

    def R(name, lo=0, hi=None, step=1):
        return (name, lo, SB[name][0] if hi is None else hi, step)

    def sub(r, lo, hi):
        return (r[0], r[1] + lo, r[1] + hi, 1)

    def tag(name, k=0):
        return (name, k, k + 1, 1)

    def ap(r):
        name, lo, hi, step = r
        return T[name][:, lo:hi] if step == 1 else T[name][:, lo:hi:step]

    def span(r):
        return (r[0], 0, 512) if r[0] in PSUM else r[:3]

    def width(r):
        return (r[2] - r[1] + r[3] - 1) // r[3]

    def two(*rs):
        return all(r[0] in SB and SB[r[0]][1] in (BF, F16, U16) for r in rs)

    def cost(in0, per, idx=None, oidx=None):
        if oidx is not None:
            return 50 + 16 * width(oidx) * EST["scat"] * CYC
        if idx is not None:
            return 60 + 16 * width(idx) * EST["gath"] * CYC
        return max(64, per * width(in0)) * CYC

    def op(q, fn, reads, writes, kind="c", **kw):
        rd = [span(r) for r in reads if r[0] not in PSUM]
        wr = [span(r) for r in writes] + [span(r) for r in reads if r[0] in PSUM]
        listed = any(r[0] in ("lst", "lvu", "msgi", "ylu") for r in reads) and writes[0][0] != "lvu"
        sort = "s" if listed and writes[0][0] == "et" else "g" if listed else "p" if q == "p" else kind
        ops.append(dict(q=q, fn=fn, rd=rd, wr=wr, kind=kind, sort=sort if kind == "c" else "", **kw))

    def sc(x):
        return ap(x) if isinstance(x, tuple) else x

    def aps(*xs):
        return [x for x in xs if isinstance(x, tuple)]

    def src(x, idx):
        return ap(x) if idx is None else ap(x).indirect(ap(idx))

    def ts(out, in0, s1, s2, o0, o1=None, idx=None):
        if o1 is None:
            f = lambda: g.vector.tensor_scalar(ap(out), src(in0, idx), sc(s1), None, o0)
        else:
            f = lambda: g.vector.tensor_scalar(ap(out), src(in0, idx), sc(s1), sc(s2), o0, o1)
        op("v", f, aps(in0, s1, s2, idx), [out], t=cost(in0, 0.5 if two(out, in0) else 1, idx))

    def tt(out, in0, in1, o, idx=None, oidx=None, extra=()):
        op("v", lambda: g.vector.tensor_tensor(src(out, oidx), src(in0, idx), ap(in1), o),
           aps(in0, in1, idx, oidx) + list(extra), [out],
           t=cost(in0, 1 if in0[0] in PSUM or in1[0] in PSUM else 2, idx, oidx))

    def cp(out, in_, idx=None):
        op("v", lambda: g.vector.tensor_copy(ap(out), src(in_, idx)), aps(in_, idx), [out],
           t=cost(in_, 0.5 if two(out, in_) else 1, idx))

    def recip(out, in_):
        op("v", lambda: g.vector.reciprocal(ap(out), ap(in_)), [in_], [out], t=190 + 6 * width(out) * CYC)

    def fill(out, c):
        op("v", lambda: g.vector.memset(ap(out), c), [], [out], t=64 * CYC)

    def act(out, in_, func=AF.Identity, bias=0.0, scale=1.0, idx=None):
        op("a", lambda: g.scalar.activation(ap(out), src(in_, idx), func, bias=sc(bias), scale=sc(scale)),
           aps(in_, bias, scale, idx), [out], t=cost(in_, 1, idx))

    def mms(out, terms, start=True, stop=True):
        k = len(terms) - 1
        op("p", lambda: [g.tensor.matmul(ap(out), ap(l), ap(r), start and i == 0, stop and i == k)
                         for i, (l, r) in enumerate(terms)][-1],
           [(x[0], x[1], x[2], 1) for t in terms for x in t], [out], t=sum(max(64, width(r)) for l, r in terms) * EST["pe"])

    def iota(out, pattern, base, cm):
        if SB[out[0]][1] == I32:
            f = lambda: g.iota(ap(out), pattern, base, cm)
        else:
            f = lambda: g.iota(ap(out), pattern, base, cm, allow_small_or_imprecise_dtypes=True)
        op("g", f, [], [out], t=130 + 2 * width(out) * CYC)

    def gcopy(out, in_):
        op("g", lambda: g.affine_select(ap(out), ap(in_), [[0, in_[2] - in_[1]]], ALU.is_ge, 0.0, 0, 0), [in_], [out],
           t=170 + 2 * width(out) * CYC)

    def dma(q, o, i, reads, writes, add=False, lat=2400):
        eng = {"g": g, "s": g.sync, "a": g.scalar}[q]
        f = (lambda: eng.dma_start(o, i, accum_op=ALU.add)) if add else (lambda: eng.dma_start(o, i))
        op(q, f, reads, writes, kind="d", t=900 if q == "g" else 100, lat=lat)

    def send(dst, srcr, sem, nbytes=2):
        op("g", lambda: g.remote_dma(ap(dst), ap(srcr), T.sem[sem], T.sem.lsent, pid, rid, out_mask), [srcr], [], kind="r",
           t=400 + 1500 * (sem == "as0"), sem=sem,
           lat=2880 + {"as0": 1500, "am0": 1000, "amsg": -300}.get(sem, 0) + width(srcr) * 128 * nbytes / EST["link"])

    def arrive(dst, sem):
        op("x", None, [], [dst], kind="x", sem=sem, t=0)

    def K(b, lo=0, hi=72):
        return (PSUM[b], lo, hi, 1)

    def ch(name, j, base=0):
        return R(name, base + CH * j, base + CH * (j + 1))

    def cols(name, lo, hi, base=0):
        return R(name, base + 16 * lo, base + 16 * hi)

    def C(i):
        return R("col", i, i + 1)

    def OH(i):
        return R("oh", i, i + 1)

    slots = {"wf": {}, "wb": {}, "col": {}, "mb16": {}, "zb": {}, "lst": {}}

    def named(buf, name, w):
        s = slots[buf]
        if name not in s:
            s[name] = sum(x[1] for x in s.values()), w
        lo, w = s[name]
        return R(buf, lo, lo + w)

    def F(name, w=1):
        return named("wf", name, 72 * w)

    def B(name, w=1):
        return named("wb", name, 72 * w)

    def C(name):
        return named("col", name, 1)

    def M(name):
        return named("mb16", name, 128)

    def Z(name):
        return named("zb", name, 144)

    def L(name):
        return named("lst", name, 72)

    def half(r, k):
        return sub(r, 72 * k, 72 * k + 72)

    def pairs(x):
        return list(zip(x[:-1], x[1:]))

    def wterms(z, data, base, lo, hi):
        return [((z[0], z[1] + 15 - i, z[1] + 143 - i, 1), R(data, base + 16 * lo + i, base + 16 * hi, 16)) for i in range(16)]

    def wrap(b, z, data, base=0, lo=0, hi=72, start=True, stop=True):
        mms(K(b, lo, hi), wterms(z, data, base, lo, hi), start, stop)

    PARTS = ((0, CFG["ha"]), (CFG["ha"], 72))
    THIRDS = ((0, 24), (24, 48), (48, 72))
    A, Bk, W0, W1 = (0, 1, 2), (3, 4, 5), 6, 7
    PF, RF, C15 = C("pf"), C("rf"), C("c15")
    DD, DN, DM = [R("dd", 128 * i, 128 * i + 128) for i in range(3)]
    JB = R("jb", 0, 128)
    slot0, slot1 = half(F("slot", 2), 0), half(F("slot"), 1)
    M0 = E + V + 80
    maskb, nmask = R("sow", E + V, E + V + 72), R("nsw", V, V + 72)

    sp0 = R("spb")
    dma("s", T.lvi[:], T.lv[:], [], [R("lvi")], lat=2600)
    dma("a", T.hdi[:], T.hd[:], [], [R("hdi")], lat=2600)
    S0 = CFG["s0"]
    dma("s", T.spb[:, 0:S0], T.sp[:, 0:S0], [], [R("spb", 0, S0)], lat=2600)
    dma("s", T.spb[:, S0:E], T.sp[:, S0:E], [], [R("spb", S0)], lat=5600)
    ops[3]["after"] = [0, 1, 2]
    send(R("nsw", V + 80, V + 80 + S0), R("spb", 0, S0), "as0")
    arrive(R("nsw", V + 80, V + 80 + S0), "as0")

    iota(R("pi", 0, 1), [[0, 1]], 0, 1)
    iota(R("jf"), [[1, 144]], 0, 0)
    iota(R("jb"), [[1, 144]], 0, 0)
    iota(R("b128"), [[128, 18]], 0, 0)
    iota(R("i16"), [[16, 72]], 0, 0)
    ts(R("pi", 1, 2), R("pi", 0, 1), 15, None, ALU.bitwise_and)
    cp(PF, R("pi", 0, 1))
    cp(RF, R("pi", 1, 2))
    ts(R("oh"), R("jf", 0, 16), RF, None, ALU.is_equal)
    ts(C15, PF, RF, 15.0, ALU.subtract, ALU.add)

    def rows(name, base, *terms):
        at = base
        for k, (r, w) in enumerate(terms):
            out = C(name) if k == len(terms) - 1 else C(name + str(k))
            act(out, OH(r), bias=at, scale=float(w))
            at = out
        return C(name)
    ts(C("k0a"), RF, 4.0, 2048.0 - BIG, ALU.is_lt, ALU.mult)
    act(C("k0b"), OH(11), bias=BIG, scale=1.0 - BIG)
    act(C("k0"), C("k0a"), bias=C("k0b"))
    act(C("set"), OH(0), scale=16.0)
    ts(R("cb1"), R("b128"), OH(1), C("k0"), ALU.mult, ALU.add)
    for b in range(9):
        act(R("et", 128 * b, 128 * b + 128), JB, bias=R("cb1", b, b + 1), scale=C("set"))
    for b in range(9, 18):
        ts(R("et", 128 * b, 128 * b + 128), JB, C("set"), R("cb1", b, b + 1), ALU.mult, ALU.add)
    for i, w in enumerate((8.0, -4.0, -2.0, -1.0)):
        ts(R("mh16", 128 * i, 128 * i + 128), JB, PF, w, ALU.is_equal, ALU.mult)
    cp(R("lvu"), R("lvi"))
    ts(R("hu", 0, 144), R("hdi"), float(MID), None, ALU.subtract)
    ts(R("hdd", 0, 144), R("hdi"), 127, None, ALU.bitwise_and)
    ts(R("hdd", 144, 288), R("hdi"), 0xF80, None, ALU.bitwise_and)
    for i, w in enumerate((512.0, 384.0, 256.0)):
        ts(R("hu", 144 * i + 144, 144 * i + 288), R("hu", 0, 144), w, -w, ALU.min, ALU.max)
    mms(K(W0, 0, 144), [(R("mh16", 128 * i, 128 * i + 128), R("hu", 144 * i, 144 * i + 144)) for i in range(4)])
    act(R("hdb", 288, 432), K(W0, 0, 144))
    cp(R("hdb", 0, 288), R("hdd"))
    for r, k in ((9, 0), (10, 1), (4, 2), (8, 2)):
        dma("s", T.et[r::16, 0:E], T.hdb[:, 144 * k:144 * k + 144], [R("hdb", 144 * k, 144 * k + 144), R("et", 0, E)], [tag("etrow", r)])
    etrows = [tag("etrow", r) for r in (9, 10, 4, 8)]
    for nm, w in (("-1", -1.0), ("1", 1.0), ("-255/256", -0.99609375), ("-15/16", -0.9375), ("1/8", 0.125), ("1/4", 0.25), ("1/2", 0.5)):
        ts(M(nm), JB, PF, w, ALU.is_equal, ALU.mult)
    rows("t47", OH(4), (7, 1))
    for s in (2, 4, 8):
        act(C("t47x%d" % s), C("t47"), scale=float(s))
    for (lo, s), (hi, _) in pairs(KNOTS):
        act(C("ctb%d" % lo), C("t47"), bias=BIG, scale=coded(lo) - BIG)
        act(R("ct", lo, hi), R("jb", 0, hi - lo), bias=C("ctb%d" % lo), scale=C("t47x%d" % s if s > 1 else "t47"))
    act(C("scc"), OH(2), scale=1 / 2048.0)
    act(C("s3"), OH(3), scale=1 / 2048.0)
    ts(R("cb3"), R("b128"), C("s3"), OH(11), ALU.mult, ALU.subtract)
    for b in range(9):
        act(R("cc", 128 * b, 128 * b + 128), JB, bias=R("cb3", b, b + 1), scale=C("scc"))
    act(slot0, R("i16"), bias=RF)
    act(slot1, slot0, bias=float(V))
    act(F("dumpk"), slot0, bias=4096.0 - E, scale=-1.0)
    ts(DD, JB, C15, 15.0, ALU.subtract, ALU.add)
    ts(DN, DD, 0.0, 200.0, ALU.is_lt, ALU.mult)
    tt(DM, DD, DN, ALU.add)
    ts(R("zh"), R("jb"), C15, None, ALU.is_equal)
    rows("w910", OH(9), (10, 1))
    rows("w23", OH(2), (3, 1))
    rows("wedge", OH(1), (0, 0.0625), (2, -1.0625))
    act(C("wh0"), C("w910"), bias=C("w23"))
    rows("wh", C("wh0"), (12, -0.25))
    for z, w in (("head", C("w910")), ("edge", C("wedge")), ("min", OH(4)), ("one", 1.0), ("vote", 4096.0), ("neg", -1.0),
                 ("h", C("wh"))):
        ts(Z(z), R("jb"), C15, w, ALU.is_equal, ALU.mult)
    rows("w78", OH(7), (8, 1))
    act(C("at4"), C("w78"), bias=RF, scale=-2.0)
    act(C("w4"), C("w78"), bias=OH(4))
    act(C("r5"), RF, bias=-5.0)
    rows("at8", C("r5"), (4, 5))
    ts(C("w8a"), RF, 4.0, None, ALU.is_ge)
    ts(C("lt9"), RF, 9.0, None, ALU.is_lt)
    act(C("w8"), C("w8a"), scale=C("lt9"))
    rows("th8", 0.0, (13, 16), (14, 5))
    rows("th4", C("th8"), (12, 4), (14, 2))
    rows("bw8", OH(13), (14, -1))
    act(C("bw4"), C("bw8"), bias=OH(12))
    ts(C("ord"), RF, 4.0, -1.0, ALU.is_gt, ALU.mult)
    act(C("ord0"), C("ord"), bias=RF)
    for k in (1, 8, 9):
        act(C("ord%d" % k), C("ord0"), bias=float(k))
    rows("pw", C("lt9"), (4, -1))
    rows("pwb", C("pw"), (8, -1))
    rows("atr", RF, (7, 1), (8, -1))
    act(C("wr0"), C("w910"), bias=1.0, scale=-1.0)
    rows("wr", C("wr0"), (11, -2))
    act(C("atc"), RF, bias=7.0)
    act(C("wc"), C("w23"), scale=2048.0)
    act(C("n7"), OH(7), scale=-1.0)
    for m, at, w in (("q4a", C("at4"), C("w4")), ("q8a", C("at8"), C("w8")), ("ea", C("ord0"), C("pw")), ("eb", C("ord8"), C("pw")),
                     ("pa", C("ord1"), C("pw")), ("pb", C("ord9"), C("pwb")), ("p4", 0.0, OH(8)), ("rev", C("atr"), C("wr")),
                     ("revc", C("atc"), C("wc"))):
        ts(M(m), DM, at, w, ALU.is_equal, ALU.mult)
    for m, below, w in (("q4b", C("th4"), C("bw4")), ("q8b", C("th8"), C("bw8")), ("ev", 16.0, C("n7")), ("sg", 16.0, OH(11))):
        ts(M(m), DM, below, w, ALU.is_lt, ALU.mult)
    tt(M("q4"), M("q4a"), M("q4b"), ALU.add)
    tt(M("q8"), M("q8a"), M("q8b"), ALU.add)
    fill(B("eps"), 2.0 ** -12)
    for rd in range(2):
        if CFG["vsv"][rd]:
            ts(B("ind%d" % rd), R("jb", 0, 72), 72.0 - CFG["vsv"][rd], -65536.0, ALU.is_ge, ALU.mult)

    XC = pairs(CFG["xc"])
    for j, (lo, hi) in enumerate(XC):
        act(cols("a16", lo, hi), sp0, scale=16.0, idx=R("lvu", 72 + lo, 72 + hi))
        tt(cols("xo", lo, hi), sp0, cols("a16", lo, hi), ALU.add, idx=R("lvu", lo, hi))
        send(cols("xn", lo, hi), cols("xo", lo, hi), "ax%d" % j)

    def xk(banks, j):
        b = at = 0
        for lo, hi in XC[:j + 1]:
            if at + 16 * (hi - lo) > 512:
                b, at = b + 1, 0
            at += 16 * (hi - lo)
        return K(banks[b], at - 16 * (hi - lo), at)
    for j, (lo, hi) in enumerate(XC):
        mms(xk(A, j), [(M("-1"), cols("xo", lo, hi)), (M("1"), cols("a16", lo, hi))])
        mms(xk(Bk, j), [(M("1"), cols("xo", lo, hi)), (M("-255/256"), cols("a16", lo, hi))])
    act(R("sow", V, E), R("a16"), scale=0.0625)
    for j, (lo, hi) in enumerate(XC):
        act(cols("sow", lo, hi), xk(A, j), scale=-1.0)
    for k in range(2):
        for lo, hi in PARTS:
            tt(cols("tab", lo, hi, V * k), R("et", 0, E), cols("ct", lo, hi), ALU.min, idx=R("lvu", 72 * k + lo, 72 * k + hi), extra=etrows)

    for j, (lo, hi) in enumerate(XC):
        arrive(cols("xn", lo, hi), "ax%d" % j)
    S1 = CFG["s1"]
    send(R("nsw", V + 80 + S0, V + 80 + S1), R("spb", S0, S1), "as1")
    ops[-1]["rd"].append(span(R("xn")))
    for j, (lo, hi) in enumerate(XC):
        tt(cols("pa16", lo, hi), xk(A, j), cols("xn", lo, hi), ALU.mult)
        ts(cols("hi", lo, hi), cols("xn", lo, hi), 1.5 * 2 ** 27, 1.5 * 2 ** 27, ALU.add, ALU.subtract)
        tt(cols("pb16", lo, hi), xk(Bk, j), cols("hi", lo, hi), ALU.mult)
    wrap(W1, R("zh"), "pa16", stop=False)
    wrap(W1, R("zh"), "pb16", start=False)
    ts(F("t0"), K(W1), 0.0, float(V), ALU.is_gt, ALU.mult)
    tt(F("lt1"), F("t0"), slot0, ALU.add)
    cp(L("t"), F("lt1"))
    act(maskb, F("t0"), scale=1.0 / V)
    fill(R("sow", E + V + 72, M0), 0.0)

    def twin(copy, out, lo, hi, how):
        who, k = how
        gcopy(cols(copy, lo, hi - k), cols(out, lo, hi - k))
        if k:
            (cp if who == "v" else act)(cols(copy, hi - k, hi), cols(out, hi - k, hi))

    def mstep(out, win, dup, idx, copy=None, how=None):
        for k, (lo, hi) in enumerate(PARTS):
            tt(cols(out, lo, hi), R(win), sub(dup, 16 * lo, 16 * hi), ALU.add, idx=sub(idx, lo, hi))
            if copy:
                twin(copy, out, lo, hi, how)

    def hop(out, win, idx, lst=None, base=0, parts=PARTS):
        whole = out in CFG["whole"]
        parts = THIRDS if out in CFG["thirds"] else parts
        for k, (lo, hi) in enumerate(parts):
            act(cols(out, lo, hi, base), win, idx=sub(idx, lo, hi))
            if lst and not whole:
                wrap((W0, W1)[k], Z("head"), out, base, lo, hi)
                cp(sub(lst, lo, hi), K((W0, W1)[k], lo, hi))
        if lst and whole:
            wrap(W1, Z("head"), out, base)
            cp(lst, K(W1))

    def merge(out, m, before, shifted):
        for j in range(3):
            mms(K(A[j], 0, CH), [(m, ch(before, j))])
            tt(ch(out, j), K(A[j], 0, CH), ch(shifted, j), ALU.min)

    def decode(b, x, lo, hi):
        for k, w in enumerate((1024.0, 512.0, 256.0)):
            ts(sub(half(x, k + 1), lo, hi), sub(x, lo, hi), w, -w, ALU.min, ALU.max)
        mms(K(b, lo, hi), [(M(w), sub(half(x, k), lo, hi)) for k, w in enumerate(("1/8", "1/8", "1/4", "1/2"))])

    def walk(rd):
        p0, b0, m5 = ("p0a", 0, "m5a") if rd == 0 else ("tab", E + V, "m5b")
        m0, c0 = ("sow", M0) if rd == 0 else ("ma", 0)
        win, tw = E + V * rd, CFG["tw"][rd]
        hop(p0, R("tab", 0, win), L("t"), L("1"), b0)
        mv = CFG["m0"][rd]
        for lo, hi in PARTS:
            for l, h, eng in ((lo, min(hi, mv), cp), (max(lo, mv), hi, act)):
                if l < h:
                    eng(cols(m0, l, h, c0), R("sow", 0, win), idx=sub(L("t"), l, h))
            if rd == 0 and lo in CFG["nega"]:
                act(cols("sow", lo, hi, E), cols(m0, lo, hi, c0), scale=-1.0)
            elif rd == 0:
                ts(cols("sow", lo, hi, E), cols(m0, lo, hi, c0), -1.0, None, ALU.mult)
            else:
                twin("ma2", "ma", lo, hi, tw[0])
        if rd == 0:
            send(R("nsw", 0, V + 80), R("sow", E, M0), "am0")
            send(R("nsw", V + 80 + S1), R("spb", S1), "as2")
        hop("p1", R(p0, b0, b0 + V), L("1"), L("2"))
        wrap(Bk[0], Z("edge"), p0, b0)
        act(F("hie"), K(Bk[0]), bias=4096.0, scale=-1.0)
        if rd == 0:
            act(F("keepk"), K(Bk[0]), bias=4096.0 - V - 80, scale=-1.0)
            for lo, hi in PARTS:
                tt(cols("mb", lo, hi), R("sow", M0, M0 + V), cols("sow", lo, hi, E), ALU.subtract, idx=sub(L("1"), lo, hi))
                twin("mb2", "mb", lo, hi, tw[1])
            for j in range(3):
                mms(K(Bk[j], 0, CH), [(M("rev"), ch(p0, j)), (M("revc"), ch("cc", j))])
                act(ch("tab", j, E), K(Bk[j], 0, CH))
        else:
            mstep("mb", "ma", R("ma2"), L("1"), "mb2", tw[1])
        hop("p2", R("p1"), L("2"), L("4"))
        mstep("ma", "mb", R("mb2"), L("2"), "ma2", tw[2])
        merge("q4", M("q4"), "p1", "p2")
        hop("p3", R("q4"), L("4"), L("8"))
        mstep("mb", "ma", R("ma2"), L("4"), "mb2", tw[3])
        merge("q8", M("q8"), "q4", "p3")
        hop("p4", R("q8"), L("8"), L("16"))
        if rd == 0:
            arrive(R("nsw", V + 80 + S0, V + 80 + S1), "as1")
            arrive(R("nsw", 0, V + 80), "am0")
            arrive(R("nsw", V + 80 + S1), "as2")
            act(F("nv"), nmask, scale=float(V))
            tt(F("yb"), F("nv"), slot0, ALU.add)
            tt(F("y2b"), slot1, F("nv"), ALU.subtract)
            tt(F("same"), maskb, nmask, ALU.is_equal)
            act(F("sm"), F("same"), bias=-FAR, scale=FAR)
            act(F("sn"), F("same"), scale=-FAR)
            act(B("hm"), nmask, bias=0.5, scale=-0.5)
        wrap(W0, Z("min"), "q8")
        act(F("e0"), K(W0))
        mstep("ma", "mb", R("mb2"), L("8"), "ma2", tw[4])
        wrap(W0, Z("min"), "p4")
        tt(F("e1"), K(W0), F("e0"), ALU.min)
        hop("p5a", R("p4"), L("8"))
        wrap(W0, Z("min"), "p5a")
        tt(F("e2"), K(W0), F("e1"), ALU.min)
        mstep(m5, "ma", R("ma2"), L("16"))
        for j in range(3):
            mms(K(A[j], 0, CH), [(M("ev"), ch(p0, j, b0))], stop=False)
            mms(K(Bk[j], 0, CH), [(M("p4"), ch("p4", j))], stop=False)
            mms(K(A[j], 0, CH), [(M("ea"), ch("p5a", j))], start=False, stop=False)
            mms(K(Bk[j], 0, CH), [(M("pa"), ch("p5a", j))], start=False, stop=False)
        pv = CFG["p5"][rd]
        for j, (lo, hi) in enumerate(THIRDS):
            for l, h, eng in ((lo, min(hi, pv), cp), (max(lo, pv), hi, act)):
                if l < h:
                    eng(cols("p5b", l, h), R("p4"), idx=sub(L("16"), l, h))
            mms(K(A[j], 0, CH), [(M("eb"), ch("p5b", j))], start=False)
            mms(K(Bk[j], 0, CH), [(M("pb"), ch("p5b", j))], start=False)
            if j in CFG["eqa"][rd]:
                act(ch("h192", j), K(A[j], 0, CH), func=AF.Abs)
                act(ch("eq", j), ch("h192", j), func=AF.Relu, bias=1.0, scale=-1.0)
            else:
                ts(ch("eq", j), K(A[j], 0, CH), 0.0, None, ALU.is_equal)
            tt(ch("pp", j), K(Bk[j], 0, CH), ch("eq", j), ALU.mult)
        cut = 72 - CFG["vsv"][rd]
        for lo, hi in pairs(CFG["lg"]):
            wrap(W1, Z("min"), "p5b", 0, lo, hi)
            tt(sub(B("x", 4), lo, hi), K(W1, lo, hi), sub(F("e2"), lo, hi), ALU.min)
            decode(W0, B("x"), lo, hi)
            ts(sub(L("l"), lo, hi), K(W0, lo, hi), float(MID), None, ALU.add)
            if lo < cut:
                act(cols("vs", lo, min(hi, cut)), R(m5), func=AF.Sign, bias=-0.5, idx=sub(L("l"), lo, min(hi, cut)))
            if hi > cut:
                ts(cols("vs", max(lo, cut), hi), R(m5), 0.0, 2.0, ALU.is_gt, ALU.mult, idx=sub(L("l"), max(lo, cut), hi))
        for k, (lo, hi) in enumerate(pairs(CFG["pg"])):
            bc, bs = (A[0], Bk[0]) if k == 0 else (A[1], Bk[1])
            mms(K(bc, lo, hi), [(M("1"), sub(B("eps"), lo, hi))] + wterms(Z("one"), "eq", 0, lo, hi))
            recip(sub(F("rc"), lo, hi), K(bc, lo, hi))
            act(sub(B("off"), lo, hi), K(bc, lo, hi), func=AF.Relu, bias=FAR, scale=-FAR)
            wrap(bs, Z("one"), "pp", 0, lo, hi)
            tt(sub(B("xp", 4), lo, hi), K(bs, lo, hi), sub(F("rc"), lo, hi), ALU.mult)
            decode(bs, B("xp"), lo, hi)
            if rd == 0:
                act(sub(F("pm"), lo, hi), K(bs, lo, hi), bias=4096.0 - MID, scale=-1.0)
            act(sub(F("pe"), lo, hi), K(bs, lo, hi), bias=float(MID + E + V * rd))
        if rd == 0:
            for j, b in enumerate((A[1], A[2], Bk[2])):
                mms(K(b, 0, CH), [(M("1"), ch("xn", j)), (M("-15/16"), ch("hi", j)), (M("1"), ch("nsw", j))])
                act(ch("no0", j), K(b, 0, CH))
        else:
            for j, b in enumerate((A[1], A[2], Bk[2])):
                mms(K(b, 0, CH), [(M("1"), ch("m5a", j)), (M("1"), ch("m5b", j))])
                act(ch("wsum", j), K(b, 0, CH))
            dma("s", T.yw[:], T.wsum[:], [R("wsum")], [tag("yw")], lat=8000)
        mms(K(W1), [(M("-1"), B("off"))] + ([(M("1"), B("ind%d" % rd))] if cut < 72 else []), stop=False)
        for lo, hi in pairs(CFG["lg"]):
            wrap(W1, Z("vote"), "vs", 0, lo, hi, start=False, stop=hi == 72)

    def pick(name, hi, lo, lst):
        tt(F(name + "u"), K(W1), hi, ALU.min)
        tt(F(name), F(name + "u"), lo, ALU.max)
        if lst:
            cp(lst, F(name))

    def edges(lst, pieces, p0, b0):
        pick("le", F("hie"), F("dumpk"), None)
        ts(lst, F("le"), -1.0, 4096.0, ALU.mult, ALU.add)
        for lo, hi in pairs(pieces):
            tt(R("et"), cols(p0, lo, hi, b0), cols("cc", lo, hi), ALU.mult, oidx=sub(lst, lo, hi))

    walk(0)
    tt(F("hy"), F("pe"), F("sm"), ALU.add)
    tt(F("hy2"), F("pe"), F("sn"), ALU.add)
    pick("sl", F("pm"), F("keepk"), None)
    ts(R("msgo"), F("sl"), -1.0, 4096.0, ALU.mult, ALU.add)
    send(R("msgi"), R("msgo"), "amsg")
    pick("y", F("hy"), F("yb"), L("y"))
    pick("y2", F("hy2"), F("y2b"), L("y2"))
    PC = pairs(CFG["pc"])
    for lo, hi in PC:
        act(cols("ys1", lo, hi), R("sow", 0, E + V), idx=sub(L("y"), lo, hi))
    for j, (lo, hi) in enumerate(THIRDS):
        if j < CFG["p2a"]:
            act(cols("h192", lo, hi), R("sow", 0, E + V), idx=sub(L("y2"), lo, hi))
            mms(K(Bk[j], 0, CH), [(M("1"), ch("no0", j))])
            tt(ch("pr2", j), K(Bk[j], 0, CH), ch("h192", j), ALU.mult)
        else:
            tt(cols("pr2", lo, hi), R("sow", 0, E + V), cols("no0", lo, hi), ALU.mult, idx=sub(L("y2"), lo, hi))
    for j, (lo, hi) in enumerate(PC[1:]):
        mms(K(A[j], 0, 16 * (hi - lo)), [(M("1"), cols("ys1", lo, hi))])
    mms(K(W0), [(M("1"), B("hm"))] + wterms(Z("neg"), "pr2", 0, 0, 72), stop=False)
    tt(F("dy"), F("y"), F("y2"), ALU.subtract)
    edges(L("e1"), CFG["sc"], "p0a", 0)
    tt(F("t1"), nmask, F("dy"), ALU.mult)
    tt(half(F("sk", 2), 0), F("y"), F("t1"), ALU.subtract)
    tt(half(F("sk"), 1), F("y2"), F("t1"), ALU.add)

    arrive(R("msgi"), "amsg")
    for j, (lo, hi) in enumerate(PC[1:]):
        act(cols("ng", lo, hi), R("nsw"), idx=R("msgi", lo, hi))
    lo, hi = PC[0]
    tt(cols("pr", lo, hi), R("nsw"), cols("ys1", lo, hi), ALU.mult, idx=R("msgi", lo, hi))
    for j, (lo, hi) in enumerate(PC[1:]):
        tt(cols("pr", lo, hi), K(A[j], 0, 16 * (hi - lo)), cols("ng", lo, hi), ALU.mult)
    wrap(W0, Z("one"), "pr", start=False)
    ts(F("pk"), K(W0), 0.0, None, ALU.is_gt)
    tt(F("t2"), F("pk"), F("dy"), ALU.mult)
    tt(F("t3"), F("t2"), F("y2"), ALU.add)
    cp(L("t"), F("t3"))
    tt(F("mk2"), F("pk"), nmask, ALU.is_equal)
    act(half(F("pen", 2), 0), F("mk2"), scale=-FAR)
    act(half(F("pen"), 1), F("mk2"), bias=-FAR, scale=FAR)
    walk(1)
    for k in range(2):
        tt(half(F("hk", 2), k), F("pe"), half(F("pen"), k), ALU.add)
    edges(L("e2"), CFG["sc2"], "tab", E + V)
    for k in range(2):
        pick("f%d" % k, half(F("hk"), k), half(F("sk"), k), R("ylu", 72 * k, 72 * k + 72))

    def rows_out(out, b, z, data, stage, extra=()):
        for lo in (0, 8):
            mms(K(b, 0, 144), [((z[0], z[1] + 15 - j, z[1] + 143 - j, 1), R(data, 144 * j, 144 * j + 144)) for j in range(lo, lo + 8)],
                lo == 0, lo == 8)
        act(stage, K(b, 0, 144))
        dma("a", out[:], ap(stage), [stage], [tag("out", b)], lat=4200 if b == W0 else 3000)
    for k in range(2):
        act(R("yg", V * k, V * k + V), R("tab"), idx=R("ylu", 72 * k, 72 * k + 72))
    rows_out(T.yl, W0, Z("edge"), "yg", F("sk"))
    lo = 0
    for j in range(6):
        mms(K(j, 0, CH), [(M("sg"), ch("et", j))])
        tt(ch("yso", j), K(j, 0, CH), ch("spb", j), ALU.mult)
        if j in CFG["ysc"]:
            dma("s", T.ys[:, CH * lo:CH * (j + 1)], T.yso[:, CH * lo:CH * (j + 1)],
                [R("yso", CH * lo, CH * (j + 1))], [tag("ys", j)], lat=2200 + 400 * (6 - lo))
            lo = j + 1
    rows_out(T.yh, W1, Z("h"), "et", F("pen"))

    emit(g, T, schedule(ops), n_in, n_out)


def meet(a, b):
    return any(x[0] == y[0] and x[1] < y[2] and y[1] < x[2] for x in a for y in b)


def clash(o, p):
    return meet(o["rd"], p["wr"]) or meet(o["wr"], p["wr"]) or meet(o["wr"], p["rd"])


ORDER = {}


def schedule(ops):
    n = len(ops)
    if n in ORDER:
        return [ops[i] for i in ORDER[n]]
    pred = [[] for _ in ops]
    succ = [[] for _ in ops]
    by = {}
    last = {}

    def gap(j, i):
        p, o = ops[j], ops[i]
        if p["kind"] == "r":
            return p["lat"] if o["kind"] == "x" else p["t"]
        if p["kind"] == "d":
            return p["lat"]
        if p["kind"] == o["kind"] == "x":
            return o["lat"]
        return p["t"] + (0 if p["q"] == o["q"] == "p" else EST["wake"])
    for i, o in enumerate(ops):
        seen = set()
        for x in o["rd"] + o["wr"]:
            seen.update(by.get(x[0], ()))
        ps = [j for j in sorted(seen) if clash(o, ops[j])]
        for x in o["rd"] + o["wr"]:
            by.setdefault(x[0], set()).add(i)
        if o["kind"] == "r":
            if "r" in last:
                ps.append(last["r"])
            last["r"] = last[o["sem"]] = i
        if o["kind"] == "x":
            ps.append(last[o["sem"]])
            if "x" in last:
                ps.append(last["x"])
            o["lat"] = ops[last[o["sem"]]]["lat"] - 2400
            last["x"] = i
        for j in o.get("after", ()):
            pred[i].append((j, ops[j]["t"]))
            succ[j].append((i, ops[j]["t"]))
        for j in ps:
            pred[i].append((j, gap(j, i)))
            succ[j].append((i, gap(j, i)))
    tail = [o["lat"] if o["kind"] == "d" else o["t"] for o in ops]

    def place(order, forward):
        start = [0.0] * n
        busy = {q: [] for q in "vapgsx"}
        for i in order:
            d = dur[i]
            if forward:
                t = 0.0
                for j, w in pred[i]:
                    if start[j] + w > t:
                        t = start[j] + w
            else:
                t = tail[i] - d
                for j, w in succ[i]:
                    if start[j] + dur[j] + w - d > t:
                        t = start[j] + dur[j] + w - d
            b = busy[que[i]]
            k = len(b)
            while k and b[k - 1][1] > t:
                k -= 1
            while k < len(b) and t + d > b[k][0]:
                t = max(t, b[k][1])
                k += 1
            b.insert(k, (t, t + d))
            start[i] = t
        return start

    state = [EST["seed"]]
    dur = [o["t"] for o in ops]
    que = [o["q"] for o in ops]
    for lst in pred + succ:
        lst[:] = list({j: max(w for k, w in lst if k == j) for j, _ in lst}.items())

    def draw():
        state[0] = (state[0] * 6364136223846793005 + 1442695040888963407) % (1 << 64)
        return (state[0] >> 33) / float(1 << 31)
    best, cur, order = None, None, list(range(n))
    for r in range(EST["rounds"]):
        for _ in range(2):
            st = place(order, True)
            end = max(st[i] + tail[i] for i in range(n))
            if best is None or end <= best[0]:
                best = (end, sorted(range(n), key=lambda i: (st[i], i)), st)
            if cur is None or end <= cur[0] + EST["heat"] * (1 - r / EST["rounds"]) * draw():
                cur = (end, st)
            back = place(sorted(range(n), key=lambda i: (-(st[i] + dur[i]), -i)), False)
            order = sorted(range(n), key=lambda i: (-(back[i] + dur[i]), i))
        t0, sig = draw() * cur[0], EST["sig"] * (0.3 + draw())
        key = [s + ((draw() + draw() + draw() - 1.5) * 2 * sig if abs(s - t0) < EST["win"] else 0.0) for s in cur[1]]
        for i in range(n):
            for j, w in pred[i]:
                if key[i] <= key[j]:
                    key[i] = key[j] + 1e-3
        order = sorted(range(n), key=lambda i: key[i])

    anc = [0] * n
    for i in range(n):
        for j, w in pred[i]:
            anc[i] |= anc[j] | 1 << j
    lean = [[(j, w) for j, w in pred[i]
             if ops[j]["kind"] != "c" or not any(anc[k] >> j & 1 and v >= EST["wake"] for k, v in pred[i])] for i in range(n)]

    cases = []
    for f in EST["cases"]:
        d = [o["t"] * f.get(o["sort"], 1.0) for o in ops]
        cases.append((d, [[(j, w - dur[j] + d[j] + f["wake"] * (w > dur[j]) if ops[j]["kind"] == "c" else w * f[ops[j]["kind"]])
                           for j, w in lean[i]] for i in range(n)]))

    def run1(seq, dur, lean):
        start, by_whom, free, on = [0.0] * n, [-1] * n, dict.fromkeys("vapgsx", 0.0), dict.fromkeys("vapgsx", -1)
        end, last_i = 0.0, 0
        for i in seq:
            q = que[i]
            t, who = free[q], on[q]
            for j, w in lean[i]:
                if start[j] + w > t:
                    t, who = start[j] + w, j
            start[i], by_whom[i], free[q], on[q] = t, who, t + dur[i], i
            if t + tail[i] > end:
                end, last_i = t + tail[i], i
        return end + sum(start) / n, start, by_whom, last_i, end

    def run(seq):
        res = [run1(seq, d, e) for d, e in cases]
        return sum(x[0] for x in res) / len(res), res[0][1], res, None, res[0][4]
    seq = best[1]
    now = run(seq)
    best = (now[0], seq)
    for r in range(EST["moves"]):
        case = now[2][int(draw() * len(cases))]
        chain, i = [], case[3] if draw() < 0.5 else int(draw() * n)
        while case[2][i] >= 0:
            j = case[2][i]
            if que[j] == que[i] and not anc[i] >> j & 1:
                chain.append((j, i))
            i = j
        if not chain:
            continue
        u, v = chain[int(draw() * len(chain))]
        a, b = seq.index(u), seq.index(v)
        hops = int(draw() ** 2 * 4)
        if draw() < 0.5:
            while hops and a > 0:
                a -= 1
                if que[seq[a]] == que[v]:
                    if anc[v] >> seq[a] & 1:
                        a += 1
                        break
                    hops -= 1
            mid = seq[a:b + 1]
            new = [x for x in mid if x == v or anc[v] >> x & 1] + [x for x in mid if x != v and not anc[v] >> x & 1]
        else:
            while hops and b < n - 1:
                b += 1
                if que[seq[b]] == que[u]:
                    if anc[seq[b]] >> u & 1:
                        b -= 1
                        break
                    hops -= 1
            mid = seq[a:b + 1]
            new = [x for x in mid if x != u and not anc[x] >> u & 1] + [x for x in mid if x == u or anc[x] >> u & 1]
        cand = seq[:a] + new + seq[b + 1:]
        res = run(cand)
        if res[0] <= now[0] + EST["heat"] * (1 - r / EST["moves"]) * draw() ** 2:
            place_of = {x: k for k, x in enumerate(cand)}
            seq, now = sorted(cand, key=lambda x: (res[1][x], place_of[x])), res
            if res[0] < best[0]:
                best = (res[0], seq)
    ORDER[n] = best[1]
    ORDER["end"] = run(best[1])[4]
    return [ops[i] for i in best[1]]


def emit(g, T, ops, n_in, n_out):
    deps = []
    by = {}
    for i, o in enumerate(ops):
        seen = set()
        for x in o["rd"] + o["wr"]:
            seen.update(by.get(x[0], ()))
        d = {}
        for j in sorted(seen, reverse=True):
            p = ops[j]
            key = p["q"] if p["kind"] == "c" else ("one", j)
            if key in d or p["kind"] == "r" or o["kind"] == "x" or (o["q"] == "p" and p["q"] == "p"):
                continue
            if clash(o, p):
                d[key] = j
        deps.append(d)
        for x in o["rd"] + o["wr"]:
            by.setdefault(x[0], set()).add(i)
    need = set()
    known = {q: {} for q in "vapgs"}
    clock = {}
    waits = []
    for i, o in enumerate(ops):
        w = []
        if o["kind"] != "x":
            k = known[o["q"]]
            for key, j in sorted(deps[i].items(), key=lambda t: -t[1]):
                if k.get(key, -1) >= j:
                    continue
                w.append(j)
                need.add(j)
                k[key] = j
                for kk, jj in clock[j].items():
                    if k.get(kk, -1) < jj:
                        k[kk] = jj
            clock[i] = dict(k)
        else:
            clock[i] = {}
        waits.append(w)
    eng = {"v": g.vector, "a": g.scalar, "p": g.tensor, "g": g, "s": g.sync}
    cnt = {q: 0 for q in "vapg"}
    mark = {}
    nd = 0
    sent = 0
    waited = {}
    for i, o in enumerate(ops):
        if o["kind"] == "x":
            mark[i] = (o["sem"], n_in)
            continue
        for j in waits[i]:
            eng[o["q"]].wait_ge(T.sem[mark[j][0]], mark[j][1])
            waited[mark[j][0]] = max(waited.get(mark[j][0], 0), mark[j][1])
        ins = o["fn"]()
        if o["kind"] == "d":
            mark[i] = ("d%d" % nd, 16)
            ins.then_inc(T.sem["d%d" % nd], 16)
            nd += 1
        elif o["kind"] == "r":
            sent += n_out
        elif i in need:
            cnt[o["q"]] += 1
            mark[i] = ("c" + o["q"], cnt[o["q"]])
            ins.then_inc(T.sem["c" + o["q"]], 1)
    g.wait_ge(T.sem.lsent, sent)
    for s, c in mark.values():
        if waited.get(s, 0) < c:
            g.wait_ge(T.sem[s], c)
            waited[s] = c
